import numpy as np, ml_dtypes
CORES = [5,29,101,125,133,157,229,253]
N = 8
import mx_ref
BF = ml_dtypes.bfloat16
def gentries(a):
    return np.ascontiguousarray(a.reshape(8, 16, -1).transpose(0, 2, 1)).reshape(8, -1)
def gtable(e):
    e = np.asarray(e); return np.ascontiguousarray(e.reshape(8, -1, 16).transpose(0, 2, 1)).reshape(128, -1).astype(np.int32)
def gcols(t, e):
    v = np.concatenate([t.reshape(8, 16, -1, 4), np.zeros((8, 16, 1, 4), BF)], axis=2)
    return np.ascontiguousarray(np.stack([v[g][:, e[g]] for g in range(8)])).reshape(128, -1)
def tile(rs):
    return np.stack(rs, axis=2).reshape(128, -1).astype(BF)
def cut(t, i, w=512):
    return t[:, w * i:w * i + w]
def pick(q, e):
    c = np.concatenate([q[0].reshape(128, -1, 4), np.zeros((128, 1, 4), np.uint8)], axis=1); s = np.concatenate([q[1], np.ones((16, 1), np.uint8)], axis=1)
    return (np.ascontiguousarray(c[:, e].reshape(128, -1)), np.ascontiguousarray(s[:, e]))
def join(*qs):
    return (np.concatenate([q[0] for q in qs], axis=1), np.concatenate([q[1] for q in qs], axis=1))
def put(q, e, v):
    c, s = q[0].reshape(128, -1, 4).copy(), q[1].copy(); c[:, e] = v[0].reshape(128, -1, 4); s[:, e] = v[1]
    return (c.reshape(128, -1), s)
def pk(c, s):
    return (np.ascontiguousarray(c), mx_ref.live(s))
def emit(q):
    return q[0], q[1]
def packed(v, rng):
    q = [mx_ref.quantize(np.ascontiguousarray(v[r])) for r in range(N)]
    return np.stack([a for a, b in q]), np.stack([mx_ref.plane(b, rng) for a, b in q])
def values_of_codes():
    e, c = np.zeros((128, 128, 4), np.float32), np.zeros((128, 2, 4), np.uint8)
    e[np.arange(128), np.arange(128), 0] = 1
    c[:127, :, 0] = np.arange(256).reshape(2, 128).T[:127]
    return mx_ref.matmul(mx_ref.quantize(e.reshape(128, 512).astype(BF)), (c.reshape(128, 8), np.full((16, 2), 127, np.uint8))).T.reshape(-1).astype(np.float64)
CODE_VALUE, SCALE_VALUE = values_of_codes(), 2.0 ** (np.arange(256) - 127.0)
def decode(q):
    return (CODE_VALUE[q[0]].reshape(16, 8, -1, 4) * SCALE_VALUE[q[1]][:, None, :, None] + 0.0).reshape(128, -1).astype(np.float32)
def f(rng, *shape):
    return mx_ref.flush((rng.standard_normal(shape, dtype=np.float32) * np.exp2(rng.integers(-2, 3, shape[:-1] + (1,)))).astype(BF))
def wide(rng, *shape, cols=0):
    v = rng.standard_normal(shape, dtype=np.float32) * np.exp2(rng.integers(-12, 13, shape)).astype(np.float32)
    if cols: v *= np.repeat(np.exp2(rng.integers(-cols, cols + 1, shape[:-2] + (1, shape[-1] // 4))) * (rng.random(shape[:-2] + (1, shape[-1] // 4)) > 0.0625), 4, axis=-1).astype(np.float32)
    return mx_ref.flush(v.astype(BF))
C, K, R = 384, 160, 3
def trim(v):
    v = np.array(v, dtype=np.float32)
    v[np.abs(v) < np.float32(2.0 ** -16)] = 0
    return v.astype(BF)
def stored(t):
    return np.stack([gtable(e) for e in t])
def numbers_of(rng):
    return {"x": trim(f(rng, N, 128, 4 * C)), "tg": stored(rng.integers(0, C, (N, 8, C))), "u": np.array(f(rng, N, 128, 512)), "v": np.array(f(rng, N, 128, 512))}
def weights(rng, w):
    c, p = packed(w, rng)
    return {"wc": c, "ws": p}
def keeping(rng, n):
    w = trim(f(rng, N, 128, 2048)).reshape(N, 8, 16, 4, 8, 16, 4)
    w[:, :, :n] = 0
    w[:, :, :, :, :, :n] = 0
    w = w.reshape(N, 128, 4, 128, 4)
    i = np.flatnonzero(np.arange(128) % 16 < n)
    for b in range(4): w[:, i, b, i, b] = 32
    return weights(rng, w.reshape(N, 128, 2048))
def signs(rng):
    return np.stack([rng.permutation(8) % 2 * 2.0 - 1.0 for r in range(N)])
def sizes(rng):
    return np.where(rng.permutation(N) < N // 2, 2.0 ** -30, 1.0).astype(np.float32)
def marked(rng, fire, late, t):
    d = numbers_of(rng)
    k = sizes(rng)
    x = d["x"].astype(np.float32).reshape(N, 8, 16, C, 4)
    x[:, :, :8] = rng.integers(8, 14, (N, 8, 8, C, 4))
    x[:, :, 0, :, 0] = 8 + (fire > 0)
    x[:, :, 0, :, 1] = 8 + (fire < 0)
    x[:, :, 1, :, 0] = 8 + (late > 0)
    x[:, :, 1, :, 1] = 8 + (late < 0)
    x[:, :, :8] *= k[:, None, None, None, None]
    u = d["u"].reshape(N, 128, 128, 4)
    for h in range(0, 128, 16):
        for i in (h, h + 1):
            u[:, :, i] = 0
            u[:, i, i, 0] = k.astype(BF)
            u[:, i, i, 1] = (-k).astype(BF)
    return {"x": x.reshape(N, 128, 4 * C).astype(BF), "tg": stored(t), "u": u.reshape(N, 128, 512), "v": d["v"], **keeping(rng, 8)}
def setup_inputs(rng):
    return {**numbers_of(rng), **weights(rng, trim(f(rng, N, 128, 2048)))}
def setup_inputs_counts(rng):
    o = rng.permutation(N)
    fire = -rng.integers(0, 2, (N, 8, C))
    late = rng.integers(-1, 2, (N, 8, C))
    t = rng.integers(0, C, (N, 8, C))
    for r in range(N):
        n = rng.permutation([K, K, K - 1, K + 1, C, 1, 0, K // 2])
        if o[r] == 0: n[:] = 0
        if o[r] == 1: n[:] = C
        for g in range(8): fire[r, g, rng.permutation(C)[:n[g]]] = 1
        a = rng.permutation(8)
        late[r, a[0]] = 1
        late[r, a[1]] = 0
        t[r, a[2]] = rng.integers(C)
        t[r, a[3]] = np.arange(C)
        t[r, a[4]] = np.arange(C) // 2
    return marked(rng, fire, late, t)
def setup_inputs_waves(rng):
    n = min(K, C // 2) // 4 * 4
    h = n // 2
    p = np.argsort(rng.random((N, 8, C)), axis=2)
    i = np.arange(C)
    z = n + np.where(i < h, i // 2, np.where(i < n, i, h + (i - n) % h))
    fire = -rng.integers(0, 2, (N, 8, C))
    late = -rng.integers(0, 2, (N, 8, C))
    t = np.zeros((N, 8, C), np.int64)
    np.put_along_axis(t, p, np.roll(p, -1, axis=0)[:, :, z], axis=2)
    np.put_along_axis(fire, p[:, :, :n], 1, axis=2)
    np.put_along_axis(late, p[:, :, h:n], 1, axis=2)
    return marked(rng, fire, late, t)
def setup_inputs_near(rng):
    d = numbers_of(rng)
    p = rng.permutation(C)
    back = np.argsort(p)
    s = p // 2
    way = 1 - s % 2 * 2
    digit = ((s[:, None] >> np.arange(8)) & 1) * np.exp2(np.arange(8) - 22.0)
    x = np.zeros((N, 8, 16, C, 4), np.float32)
    x[:, :, 0, :, 0] = 1
    x[:, :, 8] = digit[:, :4]
    x[:, :, 9] = digit[:, 4:]
    x[:, :, 10:] = rng.integers(4, 8, (N, 8, 6, C, 4)) * rng.choice([-1.0, 1.0], (N, 8, 6, C, 4)) * 2.0 ** -19
    k, sign = sizes(rng), signs(rng)
    u = d["u"].reshape(N, 128, 128, 4)
    u[:, :, ::16] = 0
    u[:, :, 1::16] = 0
    t = rng.integers(0, C, (N, 8, C))
    for g in range(8):
        h = 16 * g
        a = (k * sign[:, g]).astype(np.float32).astype(BF)
        u[:, h, h, 0] = a
        u[:, h + 8:h + 10, h] = a[:, None, None]
        u[:, h + 10, h + 1] = k.astype(BF)[:, None]
    for r in range(N):
        a = rng.permutation(8)
        a = a[np.argsort(-sign[r, a], kind="stable")]
        for i in (0, 4):
            t[r, a[i]] = np.arange(C)
            t[r, a[i + 1]] = back[(p + way) % C]
            t[r, a[i + 2]] = back[(p - way) % C]
    return {"x": x.reshape(N, 128, 4 * C).astype(BF), "tg": stored(t), "u": u.reshape(N, 128, 512), "v": d["v"], **keeping(rng, 16)}
def setup_inputs_huge(rng):
    d = numbers_of(rng)
    o = rng.permutation(N)
    g = signs(rng)
    g[o == 0] = -1
    g[o == 1] = 1
    c = np.stack([rng.permutation(C) % 2 * 2.0 - 1.0 for r in range(N)])
    c[o < 3] = 1
    x = 2.0 ** 30 * (0.6 + 0.4 * rng.random((N, 128, C, 4))) * c[:, None, :, None]
    u = d["u"].reshape(N, 128, 128, 4)
    u[:, :, ::16] = (2.0 ** 30 * (1 - 0.25 * rng.random((N, 128, 8, 4))) * g[:, None, :, None]).astype(np.float32).astype(BF)
    return {"x": x.astype(np.float32).reshape(N, 128, 4 * C).astype(BF), "tg": d["tg"], "u": u.reshape(N, 128, 512), "v": d["v"], **keeping(rng, 16)}
def setup_inputs_spread(rng):
    d = setup_inputs(rng)
    d["x"] = trim(wide(rng, N, 128, 4 * C, cols=6))
    return d
def check_inputs(d):
    b = []
    for k in ("x", "u", "v"):
        a = np.abs(d[k].astype(np.float32))
        if not (np.isfinite(a).all() and ((a == 0) | (a >= 2.0 ** -30) & (a <= 2.0 ** 30)).all()): b.append("a value of " + k)
    if ((d["tg"] < 0) | (d["tg"] >= C)).any(): b.append("an entry of tg")
    for r in range(N):
        if ((d["wc"][r] & 127) == 127).any(): b.append("wc: a code that is no number")
        if not (np.abs(decode(pk(d["wc"][r], d["ws"][r]))) <= 2.0 ** 30).all(): b.append("a number of W")
    return b
def spreadout(m):
    return np.repeat(np.repeat(m, 16, axis=0), 4, axis=1)
def reference(x, tg, u, v, wc, ws):
    qu = [mx_ref.quantize(u[r]) for r in range(N)]
    lay = [pk(wc[r], ws[r]) for r in range(N)]
    to = [gentries(tg[r]).astype(np.int64) for r in range(N)]
    now = [x[r] for r in range(N)]
    last = [np.zeros((8, C), np.float32) for r in range(N)]
    fired = [np.zeros((8, C), bool) for r in range(N)]
    kept = [[] for r in range(N)]
    due = np.full((N, R + 2, 8, C), -1)
    lists = [None] * N
    for t in range(R + 1):
        if t > 0:
            for r in range(N):
                got = gcols(np.concatenate(kept[r], axis=1), due[r, t])
                mean = ((now[r].astype(np.float32) + got.astype(np.float32)) * np.float32(0.5)).astype(BF)
                now[r] = np.where(spreadout(due[r, t] >= 0), np.where(spreadout(fired[r]), mean, got), now[r])
        if t == R: break
        sent, target, delay = [], [], []
        for r in range(N):
            s = mx_ref.matmul(qu[r], mx_ref.quantize(now[r])) + np.float32(0.0)
            rise = s[::16] > last[r]
            last[r] = s[::16]
            e = np.argsort(~rise, axis=1, kind="stable")[:, :K]
            e = np.where(np.take_along_axis(rise, e, axis=1), e, -1)
            m = np.zeros((8, C + 1), bool)
            np.put_along_axis(m, np.where(e < 0, C, e), True, axis=1)
            fired[r] = m[:, :C]
            q = mx_ref.quantize(gcols(now[r], e))
            h = tile([np.maximum(mx_ref.matmul(pick(lay[r], np.arange(128 * b, 128 * b + 128)), q), np.float32(0.0)) * np.float32(0.03125) for b in range(4)])
            sent.append(mx_ref.quantize(h))
            some = np.maximum(e, 0)
            target.append(np.take_along_axis(to[r], some, axis=1))
            delay.append(np.where(e < 0, 0, 1 + (np.take_along_axis(s[1::16], some, axis=1) > 0)))
            lists[r] = e
        came = decode(join(*sent)).astype(BF)
        for r in range(N):
            n = (r + 1) % N
            kept[n].append(cut(came, r, 4 * K))
            for w in (1, 2):
                for g in range(8):
                    k = np.flatnonzero(delay[r][g] == w)[::-1]
                    new = np.full(C, -1)
                    new[target[r][g, k]] = K * t + k
                    due[n, t + w, g] = np.where(due[n, t + w, g] < 0, new, due[n, t + w, g])
    y, ol = np.zeros((N, 128, C), np.float32), np.zeros((N, 8, K), np.float32)
    oc, osc = np.zeros((N, 128, 4 * C), np.uint8), np.zeros((N, 16, C), np.uint8)
    for r in range(N):
        q = mx_ref.quantize(now[r])
        y[r] = mx_ref.matmul(mx_ref.quantize(v[r]), q)
        ol[r] = lists[r]
        oc[r], osc[r] = emit(q)
    return {"y": y, "ol": ol, "oc": oc, "osc": osc}

@@ -1,0 +1,525 @@
+from concourse.bass import DstId, RemoteDMATransfer
+from concourse.mybir import dt, AluOpType as A, ActivationFunctionType as F, AxisListType
+
+C, K, N = 384, 160, 8
+HALF = K // 2
+M1, V1, M2, V2, WEND = 400, 560, 720, 880, 1040
+LW, LW2 = 74, 42
+F32, BF, I32, U16, COD, U8 = "float32", "bfloat16", "int32", "uint16", "float8_e4m3fn_x4", "uint8"
+SCRATCH = {}
+
+
+def _b(name, n, d, where="sbuf"):
+    SCRATCH[name] = (where, [128, n], d)
+
+
+for _t in range(4):
+    _b("XT%d" % _t, 4 * C, BF)
+    _b("xq%d" % _t, C, COD)
+    _b("xs%d" % _t, C, U8)
+    _b("EB%d" % _t, 512, BF)
+    _b("ebq%d" % _t, 128, COD)
+    _b("ebs%d" % _t, 128, U8)
+    _b("XG%d" % _t, K, BF)
+    for _k in range(1, 4):
+        _b("WB%d_%d" % (_k, _t), WEND, BF)
+for _t in range(3):
+    for _n, _w, _d in [("hq", K, COD), ("hs", K, U8), ("hl", K, COD), ("hls", K, U8), ("msg", LW, U16), ("land", LW, U16),
+                       ("rc", HALF, COD), ("rs", K, U8), ("rl", LW, U16)]:
+        _b("%s%d" % (_n, _t), _w, _d)
+for _n, _w, _d in [
+        ("UT", 512, BF), ("VT", 512, BF), ("uq", 128, COD), ("us", 128, U8), ("ur", 128, COD), ("urs", 128, U8),
+        ("ul", 128, COD), ("uls", 128, U8), ("vq", 128, COD), ("vs", 128, U8), ("wq", 512, COD), ("wsp", 512, U8),
+        ("tgT", 24, I32), ("RW", C, I32), ("RWl", C, I32), ("lanep", 1, I32), ("lanei", 1, I32), ("half", 512, BF),
+        ("vi", 24, I32), ("ET", 4 * K, BF), ("eq", K, COD), ("es", K, U8), ("HT", 4 * K, BF), ("OLr", K, F32), ("YT", C, F32)]:
+    _b(_n, _w, _d)
+PLACE, _end = {}, {}
+for _n, _w, _d in [
+        ("RWf", C, F32), ("LM", C, BF), ("tgj", 400, F32), ("LM3", 3 * C, BF), ("LMS", C, BF), ("lane", 1, F32),
+        ("lane24", 1, F32), ("i16", C, F32), ("i24", 576, F32), ("iota3", C, F32), ("iotaj", 400, F32), ("m24", 24, F32),
+        ("m16", 24, F32), ("v384", 32, F32), ("mask16", C, F32), ("nr16", C, F32), ("nr24", 576, BF), ("cT", 24, F32),
+        ("kb", 10, F32), ("kv", 10, F32), ("ce", 10, F32), ("nT", 24, F32), ("posl", 24, U16), ("lu", 8, U16),
+        ("ll", 8, U16), ("ones32", 32, F32), ("zr", C, BF), ("vb", 24, F32), ("OH", 576, BF), ("C1", 576, BF),
+        ("Hh", 32, F32), ("HT1", 32, F32), ("PI", 32, F32), ("G1", 64, F32), ("GT", 64, F32), ("BI", 32, F32),
+        ("BE", 32, F32), ("G2", 24, F32), ("DD", 576, F32), ("C2", 576, F32), ("PP", 576, F32), ("T1", 288, F32),
+        ("T2", 144, F32), ("T3", 72, F32), ("T4", 24, F32), ("T5", 24, F32), ("rk", 24, U16), ("pir", C, F32),
+        ("pim", C, F32), ("pis", C, F32), ("pi3", 24, U16), ("ne", 32, F32), ("ea", 64, F32), ("eb", 64, F32),
+        ("ec", 64, F32), ("ed", 64, F32), ("ee", 64, F32), ("endl", 2, U16), ("stl", 2, U16), ("NS", 416, BF), ("z32", 32, BF),
+        ("P0", 3 * C, BF), ("P1", 3 * C, BF), ("Z", 3 * C, BF), ("ZS", C, BF), ("SD1", 400, BF), ("SD2", 400, BF),
+        ("LAST", C, F32), ("junkS", 10 * C, BF), ("junkV", C, BF), ("acc", 10, F32), ("eh", 10, F32), ("el", 10, U16),
+        ("TT", K, F32), ("TS", K, F32), ("FM", C, F32), ("FS", C, F32), ("fv", 24, F32), ("RR", 24, F32), ("h1", 24, F32),
+        ("d0", 24, F32), ("d1", 24, F32), ("p1", 24, F32), ("h2", 24, F32), ("e0", 24, F32), ("e1", 24, F32),
+        ("p2", 24, F32), ("qf", 24, F32), ("fin", 24, U16)]:
+    PLACE[_n] = ("pack_" + _d, _end.get(_d, 0), _w)
+    _end[_d] = _end.get(_d, 0) + (_w + 31) // 32 * 32
+for _d in _end:
+    _b("pack_" + _d, _end[_d], _d)
+PSUM = ["pw0", "pw1", "pw2", "pw3", "psr", "psl", "py"]
+for _n in PSUM:
+    _b(_n, 512, F32, "psum")
+
+SEMAPHORES = (["cv", "cs", "ct", "cg", "dx", "du", "dtg", "drw", "dwc", "dws", "dv", "dol", "doc", "dos", "dy0", "dy1", "ls", "ro"]
+              + ["%s%d" % (_s, _t) for _s in ("la", "ha", "rl", "rh") for _t in range(3)])
+
+LIST_FIRST = (False, True, True)
+SCOUNT = (10, 9, 9)
+PLANES = ("vvvv", "sssv", "sssv")
+
+
+def _bits(es):
+    return sum(1 << e for e in es)
+
+
+def _relays(rank, T, topo):
+    me, dst = T.cores[rank], T.cores[(rank + 1) % N]
+    able = [c for c in topo.cores_of(me) if c != me and topo.may_write(c, dst)]
+    near = [c for c in able if topo.die(c) == topo.die(me)]
+    far = [c for c in able if topo.die(c) != topo.die(me)]
+    return near[0], far[0], near[1]
+
+
+def _relay_program(g, core, role, src, dst, T, topo):
+    rid, pid = topo.addr(dst, core)
+    mask, n_out, n_all = topo.mask(core, dst), len(topo.engines(core, dst)), len(topo.engines(src, core))
+    sent = [0]
+
+    def fwd(out, in_, sem):
+        g.remote_dma(out, in_, T.sem[sem], T.sem.ro, pid, rid, mask)
+        sent[0] += n_out
+
+    def lists(t):
+        w = LW if t < 2 else LW2
+        g.wait_ge(T.sem["rl%d" % t], n_all)
+        fwd(T["land%d" % t][:, 0:w], T["rl%d" % t][:, 0:w], "la%d" % t)
+
+    for t in range(3):
+        if role == 2 and LIST_FIRST[t]:
+            lists(t)
+        g.wait_ge(T.sem["rh%d" % t], n_all if role == 2 else n_all // 2)
+        if role == 2:
+            fwd(T["hls%d" % t][:, 0:K], T["rs%d" % t][:, 0:K], "ha%d" % t)
+        else:
+            fwd(T["hl%d" % t][:, HALF * role:HALF * role + HALF].bitcast(dt.uint8), T["rc%d" % t][:, 0:HALF].bitcast(dt.uint8), "ha%d" % t)
+        if role == 2 and not LIST_FIRST[t]:
+            lists(t)
+    g.wait_ge(T.sem.ro, sent[0])
+
+
+def rank_program(g, core, T, topo):
+    rank = T.rank_of(core)
+    if rank is None:
+        for r, c in enumerate(T.cores):
+            if core in topo.cores_of(c):
+                rel = _relays(r, T, topo)
+                if core in rel:
+                    _relay_program(g, core, rel.index(core), c, T.cores[(r + 1) % N], T, topo)
+        return
+    queue = {"v": g.vector, "s": g.scalar, "t": g.tensor, "g": g, "y": g.sync}
+    own = {"v": "cv", "s": "cs", "t": "ct", "g": "cg"}
+    total, waited, known = {}, {}, {q: {} for q in queue}
+    writer, readers = {}, {}
+
+    def deps(q, R, W):
+        evs = [writer[k] for k in R if k in writer]
+        for k in W:
+            evs += readers.get(k, []) + ([writer[k]] if k in writer else [])
+        for e in sorted(evs, key=lambda e: (-sum(e["clock"].values()), e["sem"])):
+            if known[q].get(e["sem"], 0) < e["n"]:
+                queue[q].wait_ge(T.sem[e["sem"]], e["n"])
+                waited[e["sem"]] = max(waited.get(e["sem"], 0), e["n"])
+                for s, n in e["clock"].items():
+                    known[q][s] = max(known[q].get(s, 0), n)
+
+    def note(sem, kq, R, W):
+        clock = dict(known[kq]) if kq else {}
+        clock[sem] = total[sem]
+        ev = {"sem": sem, "n": total[sem], "clock": clock}
+        for k in R:
+            readers.setdefault(k, []).append(ev)
+        for k in W:
+            writer[k], readers[k] = ev, []
+
+    def p(name, a=0, b=None, step=1, key=None):
+        buf, at, w = PLACE[name] if name in PLACE else (name, 0, SCRATCH[name][1][1])
+        return T[buf][:, at + a:at + (w if b is None else b):step], [name] if key is None else [key] if isinstance(key, str) else list(key)
+
+    def ix(win, off):
+        return win[0].indirect(off[0]), win[1] + off[1]
+
+    def cast(x, d):
+        return x[0].bitcast(d), x[1]
+
+    def op(q, fn, outs, ins):
+        R = sorted({k for o in ins for k in o[1]})
+        W = sorted({k for o in outs for k in o[1]} | {k for k in R if k in PSUM})
+        deps(q, R, W)
+        total[own[q]] = total.get(own[q], 0) + 1
+        fn().then_inc(T.sem[own[q]], 1)
+        note(own[q], q, R, W)
+
+    def dma(q, pairs, sem, R, W):
+        deps(q, R, W)
+        for o, i in pairs:
+            queue[q].dma_start(o, i).then_inc(T.sem[sem], 16)
+            total[sem] = total.get(sem, 0) + 16
+        note(sem, q, R, W)
+
+    v, s = g.vector, g.scalar
+
+    def val(x):
+        return x[0] if isinstance(x, tuple) else x
+
+    def ts(out, in0, a, o0, b=None, o1=None):
+        ins = [in0] + [x for x in (a, b) if isinstance(x, tuple)]
+        if o1 is None:
+            op("v", lambda: v.tensor_scalar(out[0], in0[0], val(a), None, o0), [out], ins)
+        else:
+            op("v", lambda: v.tensor_scalar(out[0], in0[0], val(a), val(b), o0, o1), [out], ins)
+
+    def tt(out, a, b, o):
+        op("v", lambda: v.tensor_tensor(out[0], a[0], b[0], o), [out], [a, b])
+
+    def cp(out, in_):
+        op("v", lambda: v.tensor_copy(out[0], in_[0]), [out], [in_])
+
+    def fill(out, c):
+        op("v", lambda: v.memset(out[0], c), [out], [])
+
+    def scan(out, d0, d1, init, o0, o1):
+        op("v", lambda: v.tensor_tensor_scan(out[0], d0[0], d1[0], init, o0, o1), [out], [d0, d1])
+
+    def turn(out, in_):
+        op("v", lambda: v.transpose(out[0], in_[0]), [out], [in_])
+
+    def act(out, in_, func=F.Copy, bias=None, accum=None, **kw):
+        if bias is None:
+            op("s", lambda: s.activation(out[0], in_[0], func, **kw), [out], [in_])
+        else:
+            op("s", lambda: s.activation(out[0], in_[0], func, bias=bias[0], accum_out=accum[0], **kw), [out, accum], [in_, bias])
+
+    def copy(q, out, in_):
+        (cp if q == "v" else act)(out, in_)
+
+    def quant(c, sc, in_):
+        op("v", lambda: v.quantize_mx(c[0], sc[0], in_[0]), [c, sc], [in_])
+
+    def mm(out, l, ls, r, rs):
+        op("t", lambda: g.tensor.matmul_mx(out[0], l[0], ls[0], r[0], rs[0], True, True), [out], [l, ls, r, rs])
+
+    def iota(out, pattern, base=0, ch=0):
+        op("g", lambda: g.iota(out[0], pattern, base, ch, allow_small_or_imprecise_dtypes=True), [out], [])
+
+    def XT(t, b=None):
+        return p("XT%d" % t, 0, None, 1, ["XT%d_%d" % (t, i) for i in range(4)]) if b is None else p("XT%d" % t, b, None, 4, "XT%d_%d" % (t, b))
+
+    def WB(n, b, a, e, parts):
+        return p("WB%d_%d" % (n, b), a, e, 1, ["W%s%d_%d" % (k, n, b) for k in parts])
+
+    dma("s", [(T.XT0[:, :], T.x[:, :])], "dx", [], XT(0)[1])
+    dma("y", [(T.tgT[:, :], T.tg[:, :])], "dtg", [], ["tgT"])
+    dma("y", [(T.UT[:, :], T.u[:, :])], "du", [], ["UT"])
+    dma("y", [(T.RW[i:128:16, :], T.tg[:, :]) for i in range(16)], "drw", [], ["RW"])
+    dma("y", [(T.wq[:, :].bitcast(dt.uint8), T.wc[:, :])], "dwc", [], ["wq"])
+    dma("y", [(T.wsp[:, :], T.ws[:, :])], "dws", [], ["wsp"])
+    dma("y", [(T.VT[:, :], T.v[:, :])], "dv", [], ["VT"])
+
+    iota(p("lanep"), [[1, 1]], 0, 1)
+    iota(p("m16"), [[16, 24]])
+    iota(p("m24"), [[1, 24]])
+    iota(p("i24"), [[0, 24], [1, 24]])
+    iota(p("i16"), [[0, 24], [1, 16]])
+    iota(p("v384"), [[1, 32]], C)
+    iota(p("iota3"), [[3, C]], 2)
+    iota(p("iotaj", 0, C), [[1, C]])
+    fill(p("half"), 0.5)
+    for b in range(4):
+        op("g", lambda b=b: g.affine_select(T["EB%d" % b][:, :], T.half[:, :], [[1, 512]], A.is_equal, 0.0, -b, -4), [p("EB%d" % b)], [p("half")])
+    fill(p("P1"), 0.0)
+    fill(p("P0"), 0.0)
+    fill(p("zr"), 0.0)
+    fill(p("ones32"), 1.0)
+    fill(p("Hh"), 0.0)
+    ts(p("lanei"), p("lanep"), 15, A.bitwise_and)
+    cp(p("lane"), p("lanei"))
+    cp(p("lu"), p("m16", 0, 8))
+    ts(p("ll"), p("m16", 0, 8), 1.0, A.add)
+    ts(p("lane24"), p("lane"), 24.0, A.mult)
+    ts(p("nr24"), p("i24"), 0.0, A.is_gt)
+
+    OHS = ["OH%d" % k for k in range(24)]
+    ts(p("vi"), p("tgT"), 4, A.arith_shift_right)
+    cp(p("vb"), p("vi"))
+    for k in range(24):
+        ts(p("OH", 24 * k, 24 * k + 24, 1, OHS[k]), p("vb"), float(k), A.is_equal)
+    act(p("DD"), p("OH", key=OHS))
+    scan(p("C1"), p("nr24"), p("OH", key=OHS), 0.0, A.mult, A.add)
+    quant(p("uq"), p("us"), p("UT"))
+    ts(p("nr16"), p("i16"), 0.0, A.is_gt)
+    cp(p("Hh", 0, 24), p("C1", 23, 576, 24))
+    cp(cast(p("ur"), dt.uint32), ix(cast(p("uq"), dt.uint32), p("lu")))
+    act(p("urs"), ix(p("us"), p("lu")))
+    turn(p("HT1"), p("Hh"))
+    cp(cast(p("ul"), dt.uint32), ix(cast(p("uq"), dt.uint32), p("ll")))
+    act(p("uls"), ix(p("us"), p("ll")))
+    scan(p("PI"), p("nr16", 0, 32), p("HT1"), 0.0, A.mult, A.add)
+    tt(p("G1", 0, 32), p("PI"), p("HT1"), A.subtract)
+    for a in range(2):
+        ts(p("G1", 32 + 16 * a, 48 + 16 * a, 1, "G1%d" % a), p("PI", 16 * a, 16 * a + 16), 0.0, A.mult, p("PI", 16 * a + 15, 16 * a + 16), A.add)
+    turn(p("GT"), p("G1", key=["G1", "G10", "G11"]))
+    scan(p("BI"), p("ones32"), p("GT", 32, 64), 0.0, A.mult, A.add)
+    tt(p("BE"), p("BI"), p("GT", 32, 64), A.subtract)
+    tt(p("G2"), p("GT", 0, 24), p("BE", 0, 24), A.add)
+    tt(p("DD", 0, 576, 24), p("OH", 0, 576, 24, OHS), p("G2"), A.add)
+    ts(p("kb"), p("m16", 0, 10), p("lane"), A.add, -160.5, A.add)
+    ts(p("kv"), p("m16", 0, 10), p("lane"), A.add, -161.0, A.add)
+
+    def quant_x(t):
+        quant(p("xq%d" % t), p("xs%d" % t), XT(t))
+
+    def planes(t, q):
+        for b in range(4):
+            if PLANES[t][b] == q:
+                copy(q, WB(t + 1, b, 0, C, "X"), XT(t, b))
+
+    def scores(t):
+        mm(p("psr", 0, C), p("ur"), p("urs"), p("xq%d" % t), p("xs%d" % t))
+        mm(p("psl", 0, C), p("ul"), p("uls"), p("xq%d" % t), p("xs%d" % t))
+
+    def rise(t):
+        r = p("P0", 1, None, 3, "P0r")
+        if t == 0:
+            ts(r, p("psr", 0, C), 0.0, A.is_gt)
+        else:
+            tt(r, p("psr", 0, C), p("LAST"), A.is_gt)
+        scan(p("P1", 0, None, 3, "P1y"), r, p("zr"), -161.0, A.add, A.min)
+
+    def counts(t):
+        for m in range(10):
+            y, n, a = p("P1", 48 * m, None, 3, "P1y"), C - 16 * m, p("acc", m, m + 1, 1, "acc%d" % m)
+            if m < SCOUNT[t]:
+                act(p("junkS", C * m, C * m + n, 1, "junkS%d" % m), y, F.Sign, bias=p("kb", m, m + 1), accum=a, scale=-1.0)
+            else:
+                ts(p("junkV", 0, n), y, p("kv", m, m + 1), A.is_le, 2.0, A.mult)
+                op("v", lambda: v.tensor_reduce(a[0], p("junkV", 0, n)[0], AxisListType.X, A.add), [a], [p("junkV")])
+
+    def late(t):
+        ts(p("P0", 2, None, 3, "P0l"), p("psl", 0, C), 0.0, A.is_gt, 0.5, A.subtract)
+        scan(p("Z"), p("P0", 0, None, 1, ["P0", "P0r", "P0l"]), p("P1", 0, None, 1, ["P1", "P1y"]), 0.0, A.mult, A.add)
+
+    def resolve(t):
+        m = "msg%d" % t
+        tt(p("ZS"), ix(p("Z"), p("pi3")), p("LMS"), A.mult)
+        scan(p("SD1", 0, C), p("NS", 0, C), p("ZS"), 0.0, A.mult, A.max)
+        if t < 2:
+            scan(p("SD2", 0, C), p("NS", 0, C), p("ZS"), 0.0, A.mult, A.min)
+        ts(p(m, 0, 32, 1, m + "a"), ix(p("SD1", 0, 400, 1, ["SD1", "SDp"]), p("endl")), 2.0, A.mult)
+        if t < 2:
+            ts(p(m, 42, 74, 1, m + "b"), ix(p("SD2", 0, 400, 1, ["SD2", "SDq"]), p("endl")), -2.0, A.mult)
+
+    def entries(t):
+        tt(p("eh"), p("acc", 0, 10, 1, ["acc%d" % m for m in range(10)]), p("ce"), A.add)
+        ts(p("el"), p("eh"), 0.5, A.mult)
+        for b, q in ((0, "s"), (2, "v"), (1, "s"), (3, "v")):
+            copy(q, p("ET", b, None, 4, "ET%d" % b), ix(WB(t + 1, b, 0, M1, "X0"), p("el")))
+
+    def layer(t):
+        quant(p("eq"), p("es"), p("ET", 0, None, 1, ["ET%d" % b for b in range(4)]))
+        for b in range(4):
+            mm(p("pw%d" % b, 0, K), p("wq", 128 * b, 128 * b + 128), p("wsp", 128 * b, 128 * b + 128), p("eq"), p("es"))
+
+    def targets(t):
+        tt(p("TT"), ix(p("tgj", 0, 400, 1, ["tgj", "tgjp"]), p("el")), p("mask16", 0, K), A.mult)
+        scan(p("TS"), p("nr16", 0, K), p("TT"), 0.0, A.mult, A.add)
+        cp(p("msg%d" % t, 32, 42, 1, "msg%dc" % t), p("TS", 15, K, 16))
+
+    def relus(t, on_s):
+        for b in range(4):
+            o, i = p("HT", b, None, 4, "HT%d" % b), p("pw%d" % b, 0, K)
+            if b in on_s:
+                act(o, i, F.Relu, scale=0.03125)
+            else:
+                ts(o, i, 0.0, A.max, 0.03125, A.mult)
+
+    def quant_h(t):
+        quant(p("hq%d" % t), p("hs%d" % t), p("HT", 0, None, 1, ["HT%d" % b for b in range(4)]))
+
+    rel = _relays(rank, T, topo)
+
+    def send(i, out, in_, sem):
+        rid, pid = topo.addr(rel[i], core)
+        g.remote_dma(out, in_, T.sem[sem], T.sem.ls, pid, rid, topo.mask(core, rel[i]))
+        total["ls"] = total.get("ls", 0) + len(topo.engines(core, rel[i]))
+
+    def send_codes(t):
+        deps("g", ["hq%d" % t, "hs%d" % t], [])
+        es = topo.engines(core, rel[0])
+        h, tr = len(es) // 2, []
+        for i in range(2):
+            rid, pid = topo.addr(rel[i], core)
+            tr.append(RemoteDMATransfer(dst_ids=[DstId(rid=rid, pnc=pid)], dma_engine_mask=_bits(es[h * i:h * i + h]), remote_sem=T.sem["rh%d" % t],
+                                        src=T["hq%d" % t][:, HALF * i:HALF * i + HALF].bitcast(dt.uint8), dst=T["rc%d" % t][:, 0:HALF].bitcast(dt.uint8)))
+        g.remote_dma_fused(tr, local_sem=T.sem.ls)
+        total["ls"] = total.get("ls", 0) + 2 * h
+        send(2, T["rs%d" % t][:, 0:K], T["hs%d" % t][:, 0:K], "rh%d" % t)
+
+    def send_list(t):
+        deps("g", ["msg%d%s" % (t, k) for k in "abc"], [])
+        w = LW if t < 2 else LW2
+        send(2, T["rl%d" % t][:, 0:w], T["msg%d" % t][:, 0:w], "rl%d" % t)
+
+    def between(t):
+        n = t + 1
+        if t < 2:
+            act(p("LAST"), p("psr", 0, C))
+        if n >= 2:
+            for b in range(4):
+                act(WB(n, b, M2, V2, "N"), WB(n - 1, b, M1, V1, "M"))
+        tt(p("FM"), p("Z", 2, None, 3), p("mask16"), A.mult)
+        scan(p("FS"), p("nr16"), p("FM"), 0.0, A.mult, A.add)
+        ts(p("fv"), p("FS", 15, C, 16), 0.0, A.not_equal, 160.0, A.mult)
+        if n >= 2:
+            ld = "land%d" % (t - 1)
+            ts(p("h2"), p(ld, 42, 66), 0.0, A.is_gt)
+            ts(p("e0"), p(ld, 42, 66), -1.0, A.mult, float(V2), A.add)
+            tt(p("e1"), p("e0"), p("fv"), A.add)
+            tt(p("p2"), p("e1"), p("h2"), A.mult)
+            tt(p("RR"), p("p2"), p("cT"), A.max)
+            for b in range(4):
+                tt(WB(n, b, V2, WEND, "B"), ix(WB(n, b, 0, M1, "X0"), p(ld, 32, 42)), WB(n, b, M2, V2, "N"), A.add)
+            for b in range(4):
+                ts(WB(n, b, V2, WEND, "B"), WB(n, b, V2, WEND, "B"), 0.5, A.mult)
+
+    def merge(n):
+        t = n - 1
+        ld = "land%d" % t
+        for b in (0, 2, 1, 3):
+            o, i = p("XG%d" % b), ix(WB(n, b, 0, M1, "X0"), p(ld, 32, 42))
+            if b < 2:
+                act(o, i, scale=0.5)
+            else:
+                ts(o, i, 0.5, A.mult)
+        ts(p("h1"), p(ld, 0, 24), 0.0, A.is_gt)
+        ts(p("d0"), p(ld, 0, 24), -1.0, A.mult, float(V1), A.add)
+        tt(p("d1"), p("d0"), p("fv"), A.add)
+        tt(p("p1"), p("d1"), p("h1"), A.mult)
+        tt(p("qf"), p("p1"), p("cT" if n == 1 else "RR"), A.max)
+        cp(p("fin"), p("qf"))
+        for b in range(4):
+            mm(p("pw%d" % b, 0, K), p("ebq%d" % b), p("ebs%d" % b), p("hl%d" % t), p("hls%d" % t))
+
+        def mean(b):
+            tt(WB(n, b, V1, M2, "A"), p("pw%d" % b, 0, K), p("XG%d" % b), A.add)
+
+        def move(b):
+            act(WB(n, b, M1, V1, "M"), p("pw%d" % b, 0, K), scale=2.0)
+
+        mean(0), move(1), mean(1), move(0), mean(2), move(3), mean(3), move(2)
+        for b, q in ((0, "v"), (1, "s"), (2, "v"), (3, "s")):
+            w = WB(n, b, 0, M2, "X0MA") if n == 1 else WB(n, b, 0, WEND, "X0MANB")
+            copy(q, XT(n, b), ix(w, p("fin")))
+
+    for t in range(3):
+        for sem, n, keys in (("la", 8, ["land%d" % t]), ("ha", 24, ["hl%d" % t, "hls%d" % t])):
+            total["%s%d" % (sem, t)] = n
+            note("%s%d" % (sem, t), None, [], keys)
+
+    quant_x(0)
+    scores(0)
+    scan(p("C2"), p("nr24"), p("DD"), 0.0, A.mult, A.add)
+    ts(p("nT"), p("m24"), p("lane24"), A.add)
+    cp(p("posl"), p("nT"))
+    rise(0)
+    for b in range(4):
+        for n in range(1, 4):
+            fill(WB(n, b, C, M1, "0"), 0.0)
+    planes(0, "v")
+    tt(p("PP"), p("C2"), p("OH", key=OHS), A.mult)
+    cp(p("RWf"), p("RW"))
+    tt(p("T1"), p("PP", 0, 288), p("PP", 288, 576), A.add)
+    ts(p("RWl"), p("RW"), 15, A.bitwise_and)
+    tt(p("T2"), p("T1", 0, 144), p("T1", 144, 288), A.add)
+    ts(p("LM"), p("RWl"), p("lane"), A.is_equal)
+    tt(p("T3"), p("T2", 0, 72), p("T2", 72, 144), A.add)
+    fill(p("LM3"), 0.0)
+    tt(p("T4"), p("T3", 0, 24), p("T3", 24, 48), A.add)
+    ts(p("mask16"), p("i16"), p("lane"), A.is_equal)
+    tt(p("T5"), p("T4"), p("T3", 48, 72), A.add)
+    ns = SCOUNT[0]
+    ts(p("ce", 0, ns), p("m16", 0, ns), 1.0, A.mult, 384.0, A.add)
+    ts(p("rk"), p("T5"), -1.0, A.add)
+    counts(0)
+    cp(ix(p("pir"), p("rk", key=[])), p("iota3", 0, None, 1, ["iota3", "rk"]))
+    entries(0)
+    layer(0)
+    act(p("tgj", 0, C), ix(p("RWf"), p("posl")))
+    tt(p("pim"), p("pir"), p("mask16"), A.mult)
+    relus(0, (1, 2))
+    quant_h(0)
+    send_codes(0)
+    for m in range(SCOUNT[1], ns):
+        ts(p("ce", m, m + 1), p("m16", m, m + 1), 2.0, A.mult)
+    scan(p("pis"), p("nr16"), p("pim"), 0.0, A.mult, A.add)
+    act(p("LM3", 2, None, 3), ix(p("LM"), p("posl")))
+    late(0)
+    cp(p("pi3"), p("pis", 15, C, 16))
+    act(p("LMS"), ix(p("LM3"), p("pi3")))
+    fill(p("NS"), 1.0)
+    ts(p("ne"), p("GT", 32, 64), 0.0, A.is_gt)
+    ts(p("ea", 0, 32), p("BI"), -385.0, A.add)
+    tt(p("ea", 32, 64, 1, "ea1"), p("BE"), p("v384"), A.subtract)
+    tt(p("eb", 0, 32), p("ea", 0, 32), p("ne"), A.mult)
+    tt(p("eb", 32, 64, 1, "eb1"), p("ea", 32, 64, 1, "ea1"), p("ne"), A.mult)
+    fill(p("z32"), 0.0)
+    fill(p("SD1", C, 400, 1, "SDp"), 0.0)
+    fill(p("SD2", C, 400, 1, "SDq"), 0.0)
+    fill(p("tgj", C, 400, 1, "tgjp"), 0.0)
+    ts(p("ec", 0, 32), p("eb", 0, 32), 384.0, A.add)
+    tt(p("ec", 32, 64, 1, "ec1"), p("eb", 32, 64, 1, "eb1"), p("v384"), A.add)
+    tt(p("ed"), p("ec", key=["ec", "ec1"]), p("mask16", 0, 64), A.mult)
+    scan(p("ee"), p("nr16", 0, 64), p("ed"), 0.0, A.mult, A.add)
+    cp(p("endl"), p("ee", 15, 32, 16))
+    cp(p("stl"), p("ee", 47, 64, 16))
+    cp(ix(p("NS"), p("stl", key=[])), p("z32", 0, None, 1, ["z32", "stl"]))
+    resolve(0)
+    targets(0)
+    send_list(0)
+    ts(p("cT"), p("m16"), p("lane"), A.add)
+    for b in range(4):
+        quant(p("ebq%d" % b), p("ebs%d" % b), p("EB%d" % b))
+    between(0)
+    quant(p("vq"), p("vs"), p("VT"))
+    fill(p("iotaj", C, 400, 1, "iotajp"), -1.0)
+
+    for t in (1, 2):
+        merge(t)
+        quant_x(t)
+        planes(t, "s")
+        scores(t)
+        rise(t)
+        planes(t, "v")
+        counts(t)
+        late(t)
+        resolve(t)
+        entries(t)
+        layer(t)
+        targets(t)
+        send_list(t)
+        relus(t, (0, 1, 2))
+        quant_h(t)
+        send_codes(t)
+        between(t)
+    act(p("OLr"), ix(p("iotaj", 0, 400, 1, ["iotaj", "iotajp"]), p("el")))
+    dma("y", [(T.ol[:, :], T.OLr[0:128:16, :])], "dol", ["OLr"], [])
+
+    merge(3)
+    quant_x(3)
+    dma("y", [(T.oc[:, :], T.xq3[:, :].bitcast(dt.uint8))], "doc", ["xq3"], [])
+    mm(p("py", 0, C), p("vq"), p("vs"), p("xq3"), p("xs3"))
+    dma("y", [(T.osc[4 * k:4 * k + 4, :], T.xs3[32 * k:32 * k + 4, :]) for k in range(4)], "dos", ["xs3"], [])
+    cp(p("YT", 0, 192, 1, "YT0"), p("py", 0, 192))
+    act(p("YT", 192, C, 1, "YT1"), p("py", 192, C))
+    dma("y", [(T.y[:, 0:192], T.YT[:, 0:192])], "dy0", ["YT0"], [])
+    dma("s", [(T.y[:, 192:C], T.YT[:, 192:C])], "dy1", ["YT1"], [])
+    for sem in sorted(total):
+        if waited.get(sem, 0) < total[sem]:
+            g.wait_ge(T.sem[sem], total[sem])

@@ -1,10 +1,15 @@
 from concourse.bass import DstId, RemoteDMATransfer
-from concourse.mybir import dt, AluOpType as A, ActivationFunctionType as F, AxisListType
+from concourse.mybir import dt, AluOpType as A, ActivationFunctionType as F
 
 C, K, N = 384, 160, 8
 HALF = K // 2
+CV = C + 15
+CS = C + 32
 M1, V1, M2, V2, WEND = 400, 560, 720, 880, 1040
-LW, LW2 = 74, 42
+LT = 10
+STEP = 2.0 ** -11
+R16 = 1.5 * 2.0 ** 27
+R1 = 1.5 * 2.0 ** 23
 F32, BF, I32, U16, COD, U8 = "float32", "bfloat16", "int32", "uint16", "float8_e4m3fn_x4", "uint8"
 SCRATCH = {}
 
@@ -14,56 +19,54 @@ def _b(name, n, d, where="sbuf"):
 
 
 for _t in range(4):
-    _b("XT%d" % _t, 4 * C, BF)
+    _b("XT%d" % _t, 4 * C if _t else 4 * M1, BF)
     _b("xq%d" % _t, C, COD)
     _b("xs%d" % _t, C, U8)
-    _b("EB%d" % _t, 512, BF)
     _b("ebq%d" % _t, 128, COD)
     _b("ebs%d" % _t, 128, U8)
     _b("XG%d" % _t, K, BF)
     for _k in range(1, 4):
         _b("WB%d_%d" % (_k, _t), WEND, BF)
 for _t in range(3):
-    for _n, _w, _d in [("hq", K, COD), ("hs", K, U8), ("hl", K, COD), ("hls", K, U8), ("msg", LW, U16), ("land", LW, U16),
-                       ("rc", HALF, COD), ("rs", K, U8), ("rl", LW, U16)]:
+    for _n, _w, _d in [("hq", K, COD), ("hs", K, U8), ("hl", K, COD), ("hls", K, U8), ("tm", LT, U16), ("wm", 64, BF),
+                       ("lt", LT, U16), ("lw", 64, BF), ("rc", HALF, COD), ("rs", K, U8), ("rt", LT, U16), ("rw", 64, BF)]:
         _b("%s%d" % (_n, _t), _w, _d)
 for _n, _w, _d in [
         ("UT", 512, BF), ("VT", 512, BF), ("uq", 128, COD), ("us", 128, U8), ("ur", 128, COD), ("urs", 128, U8),
         ("ul", 128, COD), ("uls", 128, U8), ("vq", 128, COD), ("vs", 128, U8), ("wq", 512, COD), ("wsp", 512, U8),
-        ("tgT", 24, I32), ("RW", C, I32), ("RWl", C, I32), ("lanep", 1, I32), ("lanei", 1, I32), ("half", 512, BF),
-        ("vi", 24, I32), ("ET", 4 * K, BF), ("eq", K, COD), ("es", K, U8), ("HT", 4 * K, BF), ("OLr", K, F32), ("YT", C, F32)]:
+        ("tgT", 24, I32), ("RW", 2 * C, BF), ("tg2s", 48, BF), ("tl", 24, I32), ("lanep", 1, I32), ("lanei", 1, I32), ("half", 516, BF),
+        ("EBW", 516, BF), ("vi", 24, I32), ("ET", 4 * K, BF), ("eq", K, COD), ("es", K, U8), ("HT", 4 * K, BF), ("OLr", K, F32),
+        ("YT", C, F32)]:
     _b(_n, _w, _d)
 PLACE, _end = {}, {}
 for _n, _w, _d in [
-        ("RWf", C, F32), ("LM", C, BF), ("tgj", 400, F32), ("LM3", 3 * C, BF), ("LMS", C, BF), ("lane", 1, F32),
-        ("lane24", 1, F32), ("i16", C, F32), ("i24", 576, F32), ("iota3", C, F32), ("iotaj", 400, F32), ("m24", 24, F32),
-        ("m16", 24, F32), ("v384", 32, F32), ("mask16", C, F32), ("nr16", C, F32), ("nr24", 576, BF), ("cT", 24, F32),
-        ("kb", 10, F32), ("kv", 10, F32), ("ce", 10, F32), ("nT", 24, F32), ("posl", 24, U16), ("lu", 8, U16),
-        ("ll", 8, U16), ("ones32", 32, F32), ("zr", C, BF), ("vb", 24, F32), ("OH", 576, BF), ("C1", 576, BF),
-        ("Hh", 32, F32), ("HT1", 32, F32), ("PI", 32, F32), ("G1", 64, F32), ("GT", 64, F32), ("BI", 32, F32),
-        ("BE", 32, F32), ("G2", 24, F32), ("DD", 576, F32), ("C2", 576, F32), ("PP", 576, F32), ("T1", 288, F32),
-        ("T2", 144, F32), ("T3", 72, F32), ("T4", 24, F32), ("T5", 24, F32), ("rk", 24, U16), ("pir", C, F32),
-        ("pim", C, F32), ("pis", C, F32), ("pi3", 24, U16), ("ne", 32, F32), ("ea", 64, F32), ("eb", 64, F32),
-        ("ec", 64, F32), ("ed", 64, F32), ("ee", 64, F32), ("endl", 2, U16), ("stl", 2, U16), ("NS", 416, BF), ("z32", 32, BF),
-        ("P0", 3 * C, BF), ("P1", 3 * C, BF), ("Z", 3 * C, BF), ("ZS", C, BF), ("SD1", 400, BF), ("SD2", 400, BF),
-        ("LAST", C, F32), ("junkS", 10 * C, BF), ("junkV", C, BF), ("acc", 10, F32), ("eh", 10, F32), ("el", 10, U16),
-        ("TT", K, F32), ("TS", K, F32), ("FM", C, F32), ("FS", C, F32), ("fv", 24, F32), ("RR", 24, F32), ("h1", 24, F32),
-        ("d0", 24, F32), ("d1", 24, F32), ("p1", 24, F32), ("h2", 24, F32), ("e0", 24, F32), ("e1", 24, F32),
-        ("p2", 24, F32), ("qf", 24, F32), ("fin", 24, U16)]:
+        ("lane", 1, F32), ("lane48", 1, F32), ("vini", 1, F32), ("thr", 1, F32), ("sc", 1, F32), ("scA", 1, F32), ("m16", 24, F32),
+        ("m24", 24, F32), ("x36", 36, F32), ("xf", 36, F32), ("q1", 36, F32), ("fl", 36, F32), ("q2", 36, F32), ("q3", 36, F32),
+        ("q4", 36, F32), ("q5", 36, F32), ("q6", 36, F32), ("RL", 36, U16), ("PL", 36, U16), ("KC", 576, BF), ("i16", CS, BF),
+        ("iota3", C, F32), ("xio", C, F32), ("IOTA", 400, F32), ("iotaj", 400, F32), ("mt16", 16, F32), ("D2", CS, BF), ("own", 16, BF),
+        ("hlf", 16, BF), ("pw", 16, F32), ("nr24", 576, BF), ("nr16", 32, F32), ("ones32", 32, F32), ("lu", 8, U16), ("ll", 8, U16),
+        ("nT", 24, F32), ("posl", 24, U16), ("posm", 24, U16), ("el4", 40, U16), ("zr", 400, BF), ("kb", 10, F32), ("ce", 10, F32),
+        ("cT", 24, F32), ("OH", 576, BF), ("C1", 576, BF), ("Hh", 32, F32), ("HT1", 32, F32), ("PI", 32, F32), ("G1", 64, F32),
+        ("GT", 64, F32), ("BI", 33, F32), ("G2", 24, F32), ("DD", 576, F32), ("C2", 576, F32), ("C2m", 576, F32), ("NOm", 576, BF),
+        ("SEL", 576, F32), ("rk", 24, U16), ("pir", CS, F32), ("pis", CS, F32), ("pi3", 26, U16), ("bx", 32, F32), ("be", 32, F32),
+        ("endl", 2, U16), ("tgx", 400, F32), ("LM3", 1200, BF), ("LMS", CS, BF), ("NS", CS, BF),
+        ("P0", 1200, BF), ("P1", 1200, BF), ("Z", 1200, BF), ("VV", 400, BF), ("RQ", 400, BF), ("PS", 400, F32), ("acc", 10, F32),
+        ("ac1", 1, F32), ("al", 1, U16), ("TA", 16, F32), ("FF", 17, F32), ("FD", 16, F32), ("eh", 10, F32), ("el", 10, U16),
+        ("ZS", CS, BF), ("SD1", CS, BF), ("SD2", CS, BF), ("LAST", C, F32), ("junkS", 10 * C, BF), ("junk1", 400, BF),
+        ("TT", K, F32), ("TS", K, F32), ("FZ", C, F32), ("FX", C, F32), ("FS", C, F32), ("fl24", 24, F32), ("fvV", 24, F32),
+        ("RR", 24, F32), ("h1", 24, F32), ("d1", 24, F32), ("p1", 24, F32), ("h2", 24, F32), ("e0", 24, F32),
+        ("e1", 24, F32), ("p2", 24, F32), ("qf", 24, F32), ("fin", 24, U16)]:
     PLACE[_n] = ("pack_" + _d, _end.get(_d, 0), _w)
     _end[_d] = _end.get(_d, 0) + (_w + 31) // 32 * 32
+SCRATCH["tg2"] = ("dram", [128, 48], BF)
 for _d in _end:
     _b("pack_" + _d, _end[_d], _d)
 PSUM = ["pw0", "pw1", "pw2", "pw3", "psr", "psl", "py"]
 for _n in PSUM:
     _b(_n, 512, F32, "psum")
 
-SEMAPHORES = (["cv", "cs", "ct", "cg", "dx", "du", "dtg", "drw", "dwc", "dws", "dv", "dol", "doc", "dos", "dy0", "dy1", "ls", "ro"]
-              + ["%s%d" % (_s, _t) for _s in ("la", "ha", "rl", "rh") for _t in range(3)])
-
-LIST_FIRST = (False, True, True)
-SCOUNT = (10, 9, 9)
-PLANES = ("vvvv", "sssv", "sssv")
+SEMAPHORES = (["cv", "cs", "ct", "cg", "dx", "du", "dtg", "dtr", "drw", "dwc", "dws", "dv", "dol", "doc", "dos", "dy0", "dy1", "ls", "ro"]
+              + ["%s%d" % (_s, _t) for _s in ("la", "lb", "ha", "rl", "rb", "rh") for _t in range(3)])
 
 
 def _bits(es):
@@ -75,7 +78,7 @@ def _relays(rank, T, topo):
     able = [c for c in topo.cores_of(me) if c != me and topo.may_write(c, dst)]
     near = [c for c in able if topo.die(c) == topo.die(me)]
     far = [c for c in able if topo.die(c) != topo.die(me)]
-    return near[0], far[0], near[1]
+    return near[0], far[0], near[1], far[1]
 
 
 def _relay_program(g, core, role, src, dst, T, topo):
@@ -87,21 +90,19 @@ def _relay_program(g, core, role, src, dst, T, topo):
         g.remote_dma(out, in_, T.sem[sem], T.sem.ro, pid, rid, mask)
         sent[0] += n_out
 
-    def lists(t):
-        w = LW if t < 2 else LW2
-        g.wait_ge(T.sem["rl%d" % t], n_all)
-        fwd(T["land%d" % t][:, 0:w], T["rl%d" % t][:, 0:w], "la%d" % t)
-
     for t in range(3):
-        if role == 2 and LIST_FIRST[t]:
-            lists(t)
-        g.wait_ge(T.sem["rh%d" % t], n_all if role == 2 else n_all // 2)
-        if role == 2:
+        if role == 3:
+            g.wait_ge(T.sem["rb%d" % t], n_all)
+            fwd(T["lt%d" % t][:, 0:LT], T["rt%d" % t][:, 0:LT], "lb%d" % t)
+            w = 64 if t < 2 else 32
+            g.wait_ge(T.sem["rl%d" % t], n_all)
+            fwd(T["lw%d" % t][:, 0:w], T["rw%d" % t][:, 0:w], "la%d" % t)
+        elif role == 2:
+            g.wait_ge(T.sem["rh%d" % t], n_all)
             fwd(T["hls%d" % t][:, 0:K], T["rs%d" % t][:, 0:K], "ha%d" % t)
         else:
+            g.wait_ge(T.sem["rh%d" % t], n_all // 2)
             fwd(T["hl%d" % t][:, HALF * role:HALF * role + HALF].bitcast(dt.uint8), T["rc%d" % t][:, 0:HALF].bitcast(dt.uint8), "ha%d" % t)
-        if role == 2 and not LIST_FIRST[t]:
-            lists(t)
     g.wait_ge(T.sem.ro, sent[0])
 
 
@@ -186,16 +187,16 @@ def rank_program(g, core, T, topo):
         op("v", lambda: v.memset(out[0], c), [out], [])
 
     def scan(out, d0, d1, init, o0, o1):
-        op("v", lambda: v.tensor_tensor_scan(out[0], d0[0], d1[0], init, o0, o1), [out], [d0, d1])
+        op("v", lambda: v.tensor_tensor_scan(out[0], d0[0], d1[0], val(init), o0, o1), [out], [d0, d1] + ([init] if isinstance(init, tuple) else []))
 
     def turn(out, in_):
         op("v", lambda: v.transpose(out[0], in_[0]), [out], [in_])
 
-    def act(out, in_, func=F.Copy, bias=None, accum=None, **kw):
-        if bias is None:
-            op("s", lambda: s.activation(out[0], in_[0], func, **kw), [out], [in_])
-        else:
-            op("s", lambda: s.activation(out[0], in_[0], func, bias=bias[0], accum_out=accum[0], **kw), [out, accum], [in_, bias])
+    def act(out, in_, func=F.Copy, **kw):
+        op("s", lambda: s.activation(out[0], in_[0], func, **kw), [out], [in_])
+
+    def signs(junk, in_, bias, accum):
+        op("s", lambda: s.activation(junk[0], in_[0], F.Sign, bias=bias[0], accum_out=accum[0], scale=-1.0), [junk, accum], [in_, bias])
 
     def copy(q, out, in_):
         (cp if q == "v" else act)(out, in_)
@@ -209,117 +210,157 @@ def rank_program(g, core, T, topo):
     def iota(out, pattern, base=0, ch=0):
         op("g", lambda: g.iota(out[0], pattern, base, ch, allow_small_or_imprecise_dtypes=True), [out], [])
 
+    def lane_scan(out, row, n):
+        scan(out, p("D2", 0, n), row, 0.0, A.mult, A.max)
+
+    def unlane(out, rows, off=0.0):
+        ts(out, rows, p("scA"), A.mult, -2048.0 - off, A.add)
+
     def XT(t, b=None):
-        return p("XT%d" % t, 0, None, 1, ["XT%d_%d" % (t, i) for i in range(4)]) if b is None else p("XT%d" % t, b, None, 4, "XT%d_%d" % (t, b))
+        return p("XT%d" % t, 0, 4 * C, 1, ["XT%d_%d" % (t, i) for i in range(4)]) if b is None else p("XT%d" % t, b, 4 * C, 4, "XT%d_%d" % (t, b))
 
     def WB(n, b, a, e, parts):
         return p("WB%d_%d" % (n, b), a, e, 1, ["W%s%d_%d" % (k, n, b) for k in parts])
 
-    dma("s", [(T.XT0[:, :], T.x[:, :])], "dx", [], XT(0)[1])
+    dma("s", [(T.XT0[:, 0:4 * C], T.x[:, :])], "dx", [], XT(0)[1])
     dma("y", [(T.tgT[:, :], T.tg[:, :])], "dtg", [], ["tgT"])
     dma("y", [(T.UT[:, :], T.u[:, :])], "du", [], ["UT"])
-    dma("y", [(T.RW[i:128:16, :], T.tg[:, :]) for i in range(16)], "drw", [], ["RW"])
     dma("y", [(T.wq[:, :].bitcast(dt.uint8), T.wc[:, :])], "dwc", [], ["wq"])
     dma("y", [(T.wsp[:, :], T.ws[:, :])], "dws", [], ["wsp"])
     dma("y", [(T.VT[:, :], T.v[:, :])], "dv", [], ["VT"])
 
-    iota(p("lanep"), [[1, 1]], 0, 1)
-    iota(p("m16"), [[16, 24]])
-    iota(p("m24"), [[1, 24]])
-    iota(p("i24"), [[0, 24], [1, 24]])
-    iota(p("i16"), [[0, 24], [1, 16]])
-    iota(p("v384"), [[1, 32]], C)
-    iota(p("iota3"), [[3, C]], 2)
-    iota(p("iotaj", 0, C), [[1, C]])
     fill(p("half"), 0.5)
-    for b in range(4):
-        op("g", lambda b=b: g.affine_select(T["EB%d" % b][:, :], T.half[:, :], [[1, 512]], A.is_equal, 0.0, -b, -4), [p("EB%d" % b)], [p("half")])
-    fill(p("P1"), 0.0)
-    fill(p("P0"), 0.0)
-    fill(p("zr"), 0.0)
-    fill(p("ones32"), 1.0)
-    fill(p("Hh"), 0.0)
+    iota(p("lanep"), [[1, 1]], 0, 1)
+    iota(p("x36"), [[16, 36]])
+    iota(p("m16"), [[16, 24]])
+    iota(p("KC"), [[1, 24], [0, 24]])
+    iota(p("i16"), [[0, 26], [1, 16]])
+    iota(p("m24"), [[1, 24]])
+    iota(p("iota3"), [[3, C]], 2)
+    iota(p("LM3"), [[0, 1200]])
+    iota(p("IOTA"), [[1, 400]])
+    iota(p("mt16"), [[16, 16]], -64)
+    op("g", lambda: g.affine_select(T.EBW[:, :], T.half[:, :], [[1, 516]], A.is_equal, 0.0, -3, -4), [p("EBW")], [p("half")])
+
     ts(p("lanei"), p("lanep"), 15, A.bitwise_and)
+    fill(p("Hh"), 0.0)
     cp(p("lane"), p("lanei"))
+    fill(p("ones32"), 1.0)
+    ts(p("xf"), p("x36"), p("lane"), A.add)
+    fill(p("nr24"), 1.0)
+    ts(p("q1"), p("xf"), 1.0 / 24, A.mult, -11.5 / 24, A.add)
+    ts(p("q3"), p("xf"), -24.0, A.mult, 552.0, A.add)
+    ts(p("fl"), p("q1"), R1, A.add, R1, A.subtract)
+    fill(p("hlf"), 0.5)
+    ts(p("q2"), p("fl"), -24.0, A.mult)
+    ts(p("q4"), p("fl"), 577.0, A.mult)
+    tt(p("q5"), p("q2"), p("xf"), A.add)
+    tt(p("q6"), p("q4"), p("q3"), A.add)
+    cp(p("RL"), p("q5"))
+    cp(p("PL"), p("q6"))
+    ts(p("nr24", 0, 576, 24), p("nr24", 0, 576, 24), 0.0, A.mult)
     cp(p("lu"), p("m16", 0, 8))
     ts(p("ll"), p("m16", 0, 8), 1.0, A.add)
-    ts(p("lane24"), p("lane"), 24.0, A.mult)
-    ts(p("nr24"), p("i24"), 0.0, A.is_gt)
-
-    OHS = ["OH%d" % k for k in range(24)]
-    ts(p("vi"), p("tgT"), 4, A.arith_shift_right)
-    cp(p("vb"), p("vi"))
-    for k in range(24):
-        ts(p("OH", 24 * k, 24 * k + 24, 1, OHS[k]), p("vb"), float(k), A.is_equal)
-    act(p("DD"), p("OH", key=OHS))
-    scan(p("C1"), p("nr24"), p("OH", key=OHS), 0.0, A.mult, A.add)
-    quant(p("uq"), p("us"), p("UT"))
-    ts(p("nr16"), p("i16"), 0.0, A.is_gt)
-    cp(p("Hh", 0, 24), p("C1", 23, 576, 24))
-    cp(cast(p("ur"), dt.uint32), ix(cast(p("uq"), dt.uint32), p("lu")))
-    act(p("urs"), ix(p("us"), p("lu")))
-    turn(p("HT1"), p("Hh"))
-    cp(cast(p("ul"), dt.uint32), ix(cast(p("uq"), dt.uint32), p("ll")))
-    act(p("uls"), ix(p("us"), p("ll")))
-    scan(p("PI"), p("nr16", 0, 32), p("HT1"), 0.0, A.mult, A.add)
-    tt(p("G1", 0, 32), p("PI"), p("HT1"), A.subtract)
-    for a in range(2):
-        ts(p("G1", 32 + 16 * a, 48 + 16 * a, 1, "G1%d" % a), p("PI", 16 * a, 16 * a + 16), 0.0, A.mult, p("PI", 16 * a + 15, 16 * a + 16), A.add)
-    turn(p("GT"), p("G1", key=["G1", "G10", "G11"]))
-    scan(p("BI"), p("ones32"), p("GT", 32, 64), 0.0, A.mult, A.add)
-    tt(p("BE"), p("BI"), p("GT", 32, 64), A.subtract)
-    tt(p("G2"), p("GT", 0, 24), p("BE", 0, 24), A.add)
-    tt(p("DD", 0, 576, 24), p("OH", 0, 576, 24, OHS), p("G2"), A.add)
+    fill(p("BI", 0, 1, 1, "BI0"), 0.0)
+    fill(p("zr"), 0.0)
+    ts(p("nr16"), p("i16", 0, 32), 0.0, A.is_gt)
     ts(p("kb"), p("m16", 0, 10), p("lane"), A.add, -160.5, A.add)
-    ts(p("kv"), p("m16", 0, 10), p("lane"), A.add, -161.0, A.add)
+    for i in range(3):
+        for o in ("P0", "P1"):
+            act(p(o, 400 * i, 400 * i + 400, 1, o), p("half", 0, 400), scale=0.0)
+    act(p("pir"), p("half", 0, CS), F.Identity, scale=0.0, bias=1.0 + (3 * C + 2) * STEP)
+
+    ts(p("tl"), p("tgT"), 15, A.bitwise_and)
+    ts(p("tg2s", 0, 24, 1, "tg2a"), p("tgT"), -192.0, A.add)
+    cp(p("tg2s", 24, 48, 1, "tg2b"), p("tl"))
+    dma("y", [(T.tg2[:, :], T.tg2s[:, :])], "dtr", ["tg2a", "tg2b"], ["tg2"])
+    dma("y", [(T.RW[i:128:16, :], T.tg2[:, :]) for i in range(16)], "drw", ["tg2"], ["RW"])
+
+    ts(p("vi"), p("tgT"), 4, A.arith_shift_right)
+    tt(p("OH"), ix(p("vi"), p("RL")), p("KC"), A.is_equal)
+    quant(p("uq"), p("us"), p("UT"))
+    act(p("urs"), ix(p("us"), p("lu")))
+    cp(cast(p("ur"), dt.uint32), ix(cast(p("uq"), dt.uint32), p("lu")))
+    quant(p("xq0"), p("xs0"), XT(0))
+    mm(p("psr", 0, C), p("ur"), p("urs"), p("xq0"), p("xs0"))
+    act(p("DD"), p("OH"))
+    act(p("NOm"), ix(p("OH"), p("PL")), F.Identity, scale=-1.0, bias=1.0)
+    scan(p("C1"), p("nr24"), p("OH"), 0.0, A.mult, A.add)
+    cp(p("Hh", 0, 24), p("C1", 23, 576, 24))
+    turn(p("HT1"), p("Hh"))
+    ts(p("P0", 1, 3 * C, 3, "P0r"), (p("psr", 0, C)[0], ["psr", "P0"]), 0.0, A.is_gt)
+    scan(p("P1", 0, 3 * C, 3, "P1y"), (p("P0", 1, 3 * C, 3)[0], ["P0r", "P1"]), p("zr", 0, C), -161.0, A.add, A.min)
+    act(p("uls"), ix(p("us"), p("ll")))
+    scan(p("PI"), p("nr16"), p("HT1"), 0.0, A.mult, A.add)
+    tt(p("G1", 0, 32), p("PI"), p("HT1"), A.subtract)
+    cp(cast(p("ul"), dt.uint32), ix(cast(p("uq"), dt.uint32), p("ll")))
+    mm(p("psl", 0, C), p("ul"), p("uls"), p("xq0"), p("xs0"))
+    for a in range(2):
+        ts(p("G1", 32 + 16 * a, 48 + 16 * a, 1, "G1%d" % a), p("ones32", 0, 16), p("PI", 16 * a + 15, 16 * a + 16), A.mult, 1.0, A.add)
+    turn(p("GT"), p("G1", key=["G1", "G10", "G11"]))
+    scan(p("BI", 1, 33), p("ones32"), p("GT", 32, 64), 0.0, A.mult, A.add)
+    tt(p("G2"), p("GT", 0, 24), p("BI", 0, 24, 1, ["BI", "BI0"]), A.add)
+    tt(p("DD", 0, 576, 24), p("DD", 0, 576, 24), p("G2"), A.add)
 
     def quant_x(t):
         quant(p("xq%d" % t), p("xs%d" % t), XT(t))
 
-    def planes(t, q):
-        for b in range(4):
-            if PLANES[t][b] == q:
-                copy(q, WB(t + 1, b, 0, C, "X"), XT(t, b))
+    def planes(t, q, bs):
+        for b in bs:
+            copy(q, WB(t + 1, b, 0, C, "X"), XT(t, b))
 
     def scores(t):
         mm(p("psr", 0, C), p("ur"), p("urs"), p("xq%d" % t), p("xs%d" % t))
         mm(p("psl", 0, C), p("ul"), p("uls"), p("xq%d" % t), p("xs%d" % t))
 
     def rise(t):
-        r = p("P0", 1, None, 3, "P0r")
-        if t == 0:
-            ts(r, p("psr", 0, C), 0.0, A.is_gt)
-        else:
-            tt(r, p("psr", 0, C), p("LAST"), A.is_gt)
-        scan(p("P1", 0, None, 3, "P1y"), r, p("zr"), -161.0, A.add, A.min)
+        tt(p("P0", 1, 3 * C, 3, "P0r"), p("psr", 0, C), p("LAST"), A.is_gt)
 
-    def counts(t):
-        for m in range(10):
-            y, n, a = p("P1", 48 * m, None, 3, "P1y"), C - 16 * m, p("acc", m, m + 1, 1, "acc%d" % m)
-            if m < SCOUNT[t]:
-                act(p("junkS", C * m, C * m + n, 1, "junkS%d" % m), y, F.Sign, bias=p("kb", m, m + 1), accum=a, scale=-1.0)
-            else:
-                ts(p("junkV", 0, n), y, p("kv", m, m + 1), A.is_le, 2.0, A.mult)
-                op("v", lambda: v.tensor_reduce(a[0], p("junkV", 0, n)[0], AxisListType.X, A.add), [a], [p("junkV")])
+    def count():
+        scan(p("P1", 0, 3 * C, 3, "P1y"), p("P0", 1, 3 * C, 3, "P0r"), p("zr", 0, C), -161.0, A.add, A.min)
 
-    def late(t):
-        ts(p("P0", 2, None, 3, "P0l"), p("psl", 0, C), 0.0, A.is_gt, 0.5, A.subtract)
-        scan(p("Z"), p("P0", 0, None, 1, ["P0", "P0r", "P0l"]), p("P1", 0, None, 1, ["P1", "P1y"]), 0.0, A.mult, A.add)
+    def entries_by_counts(lo, hi):
+        for m in range(lo, hi):
+            n = C - 16 * m
+            signs(p("junkS", C * m, C * m + n, 1, "junkS%d" % m), p("P1", 48 * m, 3 * C, 3, "P1y"), p("kb", m, m + 1), p("acc", m, m + 1, 1, "acc%d" % m))
 
-    def resolve(t):
-        m = "msg%d" % t
-        tt(p("ZS"), ix(p("Z"), p("pi3")), p("LMS"), A.mult)
-        scan(p("SD1", 0, C), p("NS", 0, C), p("ZS"), 0.0, A.mult, A.max)
-        if t < 2:
-            scan(p("SD2", 0, C), p("NS", 0, C), p("ZS"), 0.0, A.mult, A.min)
-        ts(p(m, 0, 32, 1, m + "a"), ix(p("SD1", 0, 400, 1, ["SD1", "SDp"]), p("endl")), 2.0, A.mult)
-        if t < 2:
-            ts(p(m, 42, 74, 1, m + "b"), ix(p("SD2", 0, 400, 1, ["SD2", "SDq"]), p("endl")), -2.0, A.mult)
-
-    def entries(t):
+    def counts_end():
         tt(p("eh"), p("acc", 0, 10, 1, ["acc%d" % m for m in range(10)]), p("ce"), A.add)
         ts(p("el"), p("eh"), 0.5, A.mult)
-        for b, q in ((0, "s"), (2, "v"), (1, "s"), (3, "v")):
+
+    def entries_by_runs():
+        scan(p("VV", 0, CV), p("P0", 1, 3 * CV, 3, ["P0", "P0r", "P0v"]), p("zr", 0, CV), p("vini"), A.add, A.add)
+        signs(p("junk1", 0, CV), p("VV", 0, CV), p("thr"), p("ac1"))
+        ts(p("RQ", 0, CV), p("VV", 0, CV), R16, A.add, R16, A.subtract)
+        scan(p("PS", 1, 1 + CV), p("RQ", 0, CV), p("zr", 0, CV), 0.0, A.add, A.add)
+
+    def runs_end():
+        ts(p("al"), p("ac1"), float(CV), A.add, 0.5, A.mult)
+        tt(p("TA"), ix(p("IOTA"), p("al")), p("mt16"), A.mult)
+        tt(p("FF", 1, 17), ix(p("PS", 0, 400, 1, ["PS", "PS0"]), p("al")), p("TA"), A.subtract)
+        tt(p("FD"), p("FF", 0, 16, 1, ["FF", "FF0"]), p("FF", 1, 17), A.subtract)
+        ts(p("el"), p("FD", 0, 10), 1.0 / 16, A.mult)
+
+    def late(t):
+        o = p("P0", 2, 3 * C, 3, "P0l")
+        op("s", lambda: s.activation(o[0], p("psl", 0, C)[0], F.Sign, bias=-2.0 ** -118), [o], [p("psl"), p("P0", key="P0")])
+
+    def signed():
+        n = 3 * C + 3
+        scan(p("Z", 0, n), p("P0", 0, n, 1, ["P0", "P0r", "P0v", "P0l"]), p("P1", 0, n, 1, ["P1", "P1y"]), 0.0, A.mult, A.add)
+
+    def resolve(t):
+        m = "wm%d" % t
+        tt(p("ZS"), ix(p("Z", 0, 3 * C + 3), p("pi3")), p("LMS"), A.mult)
+        scan(p("SD1"), p("NS"), p("ZS"), 0.0, A.mult, A.max)
+        if t < 2:
+            scan(p("SD2"), p("NS"), p("ZS"), 0.0, A.mult, A.min)
+        act(p(m, 0, 32, 1, m + "a"), ix(p("SD1"), p("endl")))
+        if t < 2:
+            act(p(m, 32, 64, 1, m + "b"), ix(p("SD2"), p("endl")), scale=-1.0)
+
+    def gather_e(t, pairs):
+        for b, q in pairs:
             copy(q, p("ET", b, None, 4, "ET%d" % b), ix(WB(t + 1, b, 0, M1, "X0"), p("el")))
 
     def layer(t):
@@ -327,18 +368,16 @@ def rank_program(g, core, T, topo):
         for b in range(4):
             mm(p("pw%d" % b, 0, K), p("wq", 128 * b, 128 * b + 128), p("wsp", 128 * b, 128 * b + 128), p("eq"), p("es"))
 
-    def targets(t):
-        tt(p("TT"), ix(p("tgj", 0, 400, 1, ["tgj", "tgjp"]), p("el")), p("mask16", 0, K), A.mult)
-        scan(p("TS"), p("nr16", 0, K), p("TT"), 0.0, A.mult, A.add)
-        cp(p("msg%d" % t, 32, 42, 1, "msg%dc" % t), p("TS", 15, K, 16))
+    def targets_row():
+        act(p("TT"), ix(p("tgx", 0, 400, 1, ["tgx", "tgxp"]), p("el")))
 
-    def relus(t, on_s):
+    def targets(t):
+        lane_scan(p("TS"), p("TT"), K)
+        unlane(p("tm%d" % t), p("TS", 15, K, 16))
+
+    def relus():
         for b in range(4):
-            o, i = p("HT", b, None, 4, "HT%d" % b), p("pw%d" % b, 0, K)
-            if b in on_s:
-                act(o, i, F.Relu, scale=0.03125)
-            else:
-                ts(o, i, 0.0, A.max, 0.03125, A.mult)
+            act(p("HT", b, None, 4, "HT%d" % b), p("pw%d" % b, 0, K), F.Relu, scale=0.03125)
 
     def quant_h(t):
         quant(p("hq%d" % t), p("hs%d" % t), p("HT", 0, None, 1, ["HT%d" % b for b in range(4)]))
@@ -362,48 +401,50 @@ def rank_program(g, core, T, topo):
         total["ls"] = total.get("ls", 0) + 2 * h
         send(2, T["rs%d" % t][:, 0:K], T["hs%d" % t][:, 0:K], "rh%d" % t)
 
-    def send_list(t):
-        deps("g", ["msg%d%s" % (t, k) for k in "abc"], [])
-        w = LW if t < 2 else LW2
-        send(2, T["rl%d" % t][:, 0:w], T["msg%d" % t][:, 0:w], "rl%d" % t)
+    def send_targets(t):
+        deps("g", ["tm%d" % t], [])
+        send(3, T["rt%d" % t][:, 0:LT], T["tm%d" % t][:, 0:LT], "rb%d" % t)
+
+    def send_winners(t):
+        deps("g", ["wm%d%s" % (t, k) for k in "ab"], [])
+        w = 64 if t < 2 else 32
+        send(3, T["rw%d" % t][:, 0:w], T["wm%d" % t][:, 0:w], "rl%d" % t)
 
     def between(t):
         n = t + 1
-        if t < 2:
-            act(p("LAST"), p("psr", 0, C))
+        act(p("FZ"), p("Z", 2, 3 * C, 3), F.Abs)
+        act(p("FX"), p("FZ"), F.Identity, scale=2.0 ** -8, bias=1.0)
         if n >= 2:
+            lw = "lw%d" % (t - 1)
+            ts(p("h2"), p(lw, 32, 56), 0.0, A.is_gt)
+            ts(p("e0"), p(lw, 32, 56), -1.0, A.mult, float(V2 - V1), A.add)
             for b in range(4):
-                act(WB(n, b, M2, V2, "N"), WB(n - 1, b, M1, V1, "M"))
-        tt(p("FM"), p("Z", 2, None, 3), p("mask16"), A.mult)
-        scan(p("FS"), p("nr16"), p("FM"), 0.0, A.mult, A.add)
-        ts(p("fv"), p("FS", 15, C, 16), 0.0, A.not_equal, 160.0, A.mult)
-        if n >= 2:
-            ld = "land%d" % (t - 1)
-            ts(p("h2"), p(ld, 42, 66), 0.0, A.is_gt)
-            ts(p("e0"), p(ld, 42, 66), -1.0, A.mult, float(V2), A.add)
-            tt(p("e1"), p("e0"), p("fv"), A.add)
-            tt(p("p2"), p("e1"), p("h2"), A.mult)
-            tt(p("RR"), p("p2"), p("cT"), A.max)
-            for b in range(4):
-                tt(WB(n, b, V2, WEND, "B"), ix(WB(n, b, 0, M1, "X0"), p(ld, 32, 42)), WB(n, b, M2, V2, "N"), A.add)
+                tt(WB(n, b, V2, WEND, "B"), ix(WB(n, b, 0, M1, "X0"), p("lt%d" % (t - 1))), WB(n, b, M2, V2, "N"), A.add)
             for b in range(4):
                 ts(WB(n, b, V2, WEND, "B"), WB(n, b, V2, WEND, "B"), 0.5, A.mult)
+        if t < 2:
+            act(p("LAST"), p("psr", 0, C))
+        lane_scan(p("FS"), p("FX"), C)
+        ts(p("fl24"), p("FS", 15, C, 16), p("sc"), A.mult, 1.0, A.is_gt)
+        ts(p("fvV"), p("fl24"), 160.0, A.mult, float(V1), A.add)
+        if n >= 2:
+            tt(p("e1"), p("e0"), p("fvV"), A.add)
+            tt(p("p2"), p("e1"), p("h2"), A.mult)
+            tt(p("RR"), p("p2"), p("cT"), A.max)
+
+    def older(n):
+        for b in range(4):
+            act(WB(n, b, M2, V2, "N"), WB(n - 1, b, M1, V1, "M"))
 
     def merge(n):
         t = n - 1
-        ld = "land%d" % t
+        lw, lt = "lw%d" % t, "lt%d" % t
         for b in (0, 2, 1, 3):
-            o, i = p("XG%d" % b), ix(WB(n, b, 0, M1, "X0"), p(ld, 32, 42))
+            o, i = p("XG%d" % b), ix(WB(n, b, 0, M1, "X0"), p(lt))
             if b < 2:
                 act(o, i, scale=0.5)
             else:
                 ts(o, i, 0.5, A.mult)
-        ts(p("h1"), p(ld, 0, 24), 0.0, A.is_gt)
-        ts(p("d0"), p(ld, 0, 24), -1.0, A.mult, float(V1), A.add)
-        tt(p("d1"), p("d0"), p("fv"), A.add)
-        tt(p("p1"), p("d1"), p("h1"), A.mult)
-        tt(p("qf"), p("p1"), p("cT" if n == 1 else "RR"), A.max)
-        cp(p("fin"), p("qf"))
         for b in range(4):
             mm(p("pw%d" % b, 0, K), p("ebq%d" % b), p("ebs%d" % b), p("hl%d" % t), p("hls%d" % t))
 
@@ -413,100 +454,111 @@ def rank_program(g, core, T, topo):
         def move(b):
             act(WB(n, b, M1, V1, "M"), p("pw%d" % b, 0, K), scale=2.0)
 
-        mean(0), move(1), mean(1), move(0), mean(2), move(3), mean(3), move(2)
+        def final():
+            act(p("h1"), p(lw, 0, 24), F.Sign)
+            tt(p("d1"), p("fvV"), p(lw, 0, 24), A.subtract)
+            tt(p("p1"), p("d1"), p("h1"), A.mult)
+            tt(p("qf"), p("p1"), p("cT" if n == 1 else "RR"), A.max)
+            cp(p("fin"), p("qf"))
+
+        mean(0), move(1), mean(1), move(0)
+        final()
+        mean(2), move(3), mean(3), move(2)
         for b, q in ((0, "v"), (1, "s"), (2, "v"), (3, "s")):
             w = WB(n, b, 0, M2, "X0MA") if n == 1 else WB(n, b, 0, WEND, "X0MANB")
             copy(q, XT(n, b), ix(w, p("fin")))
 
     for t in range(3):
-        for sem, n, keys in (("la", 8, ["land%d" % t]), ("ha", 24, ["hl%d" % t, "hls%d" % t])):
+        for sem, n, keys in (("lb", 8, ["lt%d" % t]), ("la", 8, ["lw%d" % t]), ("ha", 24, ["hl%d" % t, "hls%d" % t])):
             total["%s%d" % (sem, t)] = n
             note("%s%d" % (sem, t), None, [], keys)
 
-    quant_x(0)
-    scores(0)
     scan(p("C2"), p("nr24"), p("DD"), 0.0, A.mult, A.add)
-    ts(p("nT"), p("m24"), p("lane24"), A.add)
+    act(p("xio"), p("iota3"), F.Identity, scale=STEP, bias=1.0)
+    entries_by_counts(0, 3)
+    act(p("C2m"), ix(p("C2"), p("PL")))
+    entries_by_counts(3, 10)
+    late(0)
+    ts(p("ce"), p("m16", 0, 10), 384.0, A.add)
+    ts(p("lane48"), p("lane"), 48.0, A.mult)
+    ts(p("nT"), p("m24"), p("lane48"), A.add)
     cp(p("posl"), p("nT"))
-    rise(0)
-    for b in range(4):
-        for n in range(1, 4):
-            fill(WB(n, b, C, M1, "0"), 0.0)
-    planes(0, "v")
-    tt(p("PP"), p("C2"), p("OH", key=OHS), A.mult)
-    cp(p("RWf"), p("RW"))
-    tt(p("T1"), p("PP", 0, 288), p("PP", 288, 576), A.add)
-    ts(p("RWl"), p("RW"), 15, A.bitwise_and)
-    tt(p("T2"), p("T1", 0, 144), p("T1", 144, 288), A.add)
-    ts(p("LM"), p("RWl"), p("lane"), A.is_equal)
-    tt(p("T3"), p("T2", 0, 72), p("T2", 72, 144), A.add)
-    fill(p("LM3"), 0.0)
-    tt(p("T4"), p("T3", 0, 24), p("T3", 24, 48), A.add)
-    ts(p("mask16"), p("i16"), p("lane"), A.is_equal)
-    tt(p("T5"), p("T4"), p("T3", 48, 72), A.add)
-    ns = SCOUNT[0]
-    ts(p("ce", 0, ns), p("m16", 0, ns), 1.0, A.mult, 384.0, A.add)
-    ts(p("rk"), p("T5"), -1.0, A.add)
-    counts(0)
-    cp(ix(p("pir"), p("rk", key=[])), p("iota3", 0, None, 1, ["iota3", "rk"]))
-    entries(0)
+    ts(p("posm"), p("nT"), 24.0, A.add)
+    ts(p("D2"), p("i16"), p("lane"), A.not_equal, 2.0, A.mult)
+    ts(p("own"), p("i16", 0, 16), p("lane"), A.is_equal)
+    scan(p("pw"), p("hlf"), p("own"), 0.0, A.mult, A.max)
+    cp(p("sc"), p("pw", 15, 16))
+    ts(p("scA"), p("sc"), 2048.0, A.mult)
+    fill(p("tgx", C, 400, 1, "tgxp"), 1.0)
+    fill(p("XT0", 4 * C, 4 * M1, 1, "XT0z"), 0.0)
+    ts(p("tgx", 0, C), ix(p("RW"), p("posl")), STEP, A.mult, 1.0 + 192 * STEP, A.add)
+    scan(p("SEL"), p("NOm"), p("C2m"), 0.0, A.mult, A.max)
+    cp(p("rk"), p("SEL", 23, 576, 24))
+    cp(ix(p("pir"), p("rk")), p("xio"))
+    counts_end()
+    for b, q in ((0, "s"), (2, "v"), (1, "s"), (3, "v")):
+        ts(p("el4", 10 * b, 10 * b + 10, 1, "el4%d" % b), p("eh"), 2.0, A.mult, float(b), A.add)
+        w = p("XT0", 0, 4 * M1, 1, XT(0)[1] + ["XT0z"])
+        copy(q, p("ET", b, None, 4, "ET%d" % b), ix(w, p("el4", 10 * b, 10 * b + 10, 1, "el4%d" % b)))
+    targets_row()
     layer(0)
-    act(p("tgj", 0, C), ix(p("RWf"), p("posl")))
-    tt(p("pim"), p("pir"), p("mask16"), A.mult)
-    relus(0, (1, 2))
+    targets(0)
+    send_targets(0)
+    cp(p("LM3", 2, 3 * C, 3), ix(p("RW"), p("posm")))
+    relus()
+    op("s", lambda: s.activation(p("NS")[0], p("pir")[0], F.Sign, scale=-1.0, bias=1.0 + (3 * C + 1) * STEP), [p("NS")], [p("pir")])
     quant_h(0)
     send_codes(0)
-    for m in range(SCOUNT[1], ns):
-        ts(p("ce", m, m + 1), p("m16", m, m + 1), 2.0, A.mult)
-    scan(p("pis"), p("nr16"), p("pim"), 0.0, A.mult, A.add)
-    act(p("LM3", 2, None, 3), ix(p("LM"), p("posl")))
-    late(0)
-    cp(p("pi3"), p("pis", 15, C, 16))
-    act(p("LMS"), ix(p("LM3"), p("pi3")))
-    fill(p("NS"), 1.0)
-    ts(p("ne"), p("GT", 32, 64), 0.0, A.is_gt)
-    ts(p("ea", 0, 32), p("BI"), -385.0, A.add)
-    tt(p("ea", 32, 64, 1, "ea1"), p("BE"), p("v384"), A.subtract)
-    tt(p("eb", 0, 32), p("ea", 0, 32), p("ne"), A.mult)
-    tt(p("eb", 32, 64, 1, "eb1"), p("ea", 32, 64, 1, "ea1"), p("ne"), A.mult)
-    fill(p("z32"), 0.0)
-    fill(p("SD1", C, 400, 1, "SDp"), 0.0)
-    fill(p("SD2", C, 400, 1, "SDq"), 0.0)
-    fill(p("tgj", C, 400, 1, "tgjp"), 0.0)
-    ts(p("ec", 0, 32), p("eb", 0, 32), 384.0, A.add)
-    tt(p("ec", 32, 64, 1, "ec1"), p("eb", 32, 64, 1, "eb1"), p("v384"), A.add)
-    tt(p("ed"), p("ec", key=["ec", "ec1"]), p("mask16", 0, 64), A.mult)
-    scan(p("ee"), p("nr16", 0, 64), p("ed"), 0.0, A.mult, A.add)
-    cp(p("endl"), p("ee", 15, 32, 16))
-    cp(p("stl"), p("ee", 47, 64, 16))
-    cp(ix(p("NS"), p("stl", key=[])), p("z32", 0, None, 1, ["z32", "stl"]))
+    lane_scan(p("pis"), p("pir"), CS)
+    unlane(p("pi3"), p("pis", 15, CS, 16))
+    ts(p("bx"), p("BI", 1, 33), STEP, A.mult, 1.0, A.add)
+    lane_scan(p("be"), p("bx"), 32)
+    unlane(p("endl"), p("be", 15, 32, 16), 1.0)
+    ts(p("LMS"), ix(p("LM3", 0, 3 * C + 3), p("pi3")), p("lane"), A.is_equal)
+    signed()
     resolve(0)
-    targets(0)
-    send_list(0)
+    send_winners(0)
+    for n in range(1, 4):
+        for b in range(4):
+            fill(WB(n, b, C, M1, "0"), 0.0)
+    planes(0, "s", (0, 1))
+    planes(0, "v", (2, 3))
+    ts(p("vini"), p("lane"), -1.0, A.mult, -72.5, A.add)
+    ts(p("thr"), p("lane"), 15.0, A.mult, -57.0, A.add)
+    fill(p("PS", 0, 1, 1, "PS0"), 0.0)
+    fill(p("FF", 0, 1, 1, "FF0"), 0.0)
     ts(p("cT"), p("m16"), p("lane"), A.add)
     for b in range(4):
-        quant(p("ebq%d" % b), p("ebs%d" % b), p("EB%d" % b))
+        quant(p("ebq%d" % b), p("ebs%d" % b), p("EBW", 3 - b, 515 - b))
     between(0)
+    ts(p("P0", 3 * C + 1, 3 * CV, 3, "P0v"), p("m24", 0, 15), 0.0, A.mult, 1.0, A.add)
     quant(p("vq"), p("vs"), p("VT"))
+    act(p("iotaj", 0, C), p("IOTA", 0, C))
     fill(p("iotaj", C, 400, 1, "iotajp"), -1.0)
 
     for t in (1, 2):
         merge(t)
         quant_x(t)
-        planes(t, "s")
+        planes(t, "s", (0, 1))
         scores(t)
+        planes(t, "v", (2, 3))
         rise(t)
-        planes(t, "v")
-        counts(t)
+        entries_by_runs()
         late(t)
-        resolve(t)
-        entries(t)
+        runs_end()
+        gather_e(t, ((0, "s"), (2, "v"), (1, "s"), (3, "v")))
+        targets_row()
         layer(t)
+        count()
         targets(t)
-        send_list(t)
-        relus(t, (0, 1, 2))
+        send_targets(t)
+        relus()
+        older(t + 1)
+        signed()
         quant_h(t)
         send_codes(t)
+        resolve(t)
+        send_winners(t)
         between(t)
     act(p("OLr"), ix(p("iotaj", 0, 400, 1, ["iotaj", "iotajp"]), p("el")))
     dma("y", [(T.ol[:, :], T.OLr[0:128:16, :])], "dol", ["OLr"], [])

@@ -5,10 +5,11 @@ C, K, N = 384, 160, 8
 HALF = K // 2
 CV = C + 15
 CS = C + 32
-M1, V1, M2, V2, WEND = 400, 560, 720, 880, 1040
+MID = 208
+NZ = 4 * C + 4
+M1, V1, WEND = 400, 560, 1360
 LT = 10
 STEP = 2.0 ** -11
-R16 = 1.5 * 2.0 ** 27
 R1 = 1.5 * 2.0 ** 23
 F32, BF, I32, U16, COD, U8 = "float32", "bfloat16", "int32", "uint16", "float8_e4m3fn_x4", "uint8"
 SCRATCH = {}
@@ -19,14 +20,14 @@ def _b(name, n, d, where="sbuf"):
 
 
 for _t in range(4):
-    _b("XT%d" % _t, 4 * C if _t else 4 * M1, BF)
+    _b("XT%d" % _t, 4 * C, BF)
     _b("xq%d" % _t, C, COD)
     _b("xs%d" % _t, C, U8)
     _b("ebq%d" % _t, 128, COD)
     _b("ebs%d" % _t, 128, U8)
     _b("XG%d" % _t, K, BF)
-    for _k in range(1, 4):
-        _b("WB%d_%d" % (_k, _t), WEND, BF)
+    _b("XD%d" % _t, K, BF)
+    _b("WB%d" % _t, WEND, BF)
 for _t in range(3):
     for _n, _w, _d in [("hq", K, COD), ("hs", K, U8), ("hl", K, COD), ("hls", K, U8), ("tm", LT, U16), ("wm", 64, BF),
                        ("lt", LT, U16), ("lw", 64, BF), ("rc", HALF, COD), ("rs", K, U8), ("rt", LT, U16), ("rw", 64, BF)]:
@@ -43,30 +44,30 @@ for _n, _w, _d in [
         ("lane", 1, F32), ("lane48", 1, F32), ("vini", 1, F32), ("thr", 1, F32), ("sc", 1, F32), ("scA", 1, F32), ("m16", 24, F32),
         ("m24", 24, F32), ("x36", 36, F32), ("xf", 36, F32), ("q1", 36, F32), ("fl", 36, F32), ("q2", 36, F32), ("q3", 36, F32),
         ("q4", 36, F32), ("q5", 36, F32), ("q6", 36, F32), ("RL", 36, U16), ("PL", 36, U16), ("KC", 576, BF), ("i16", CS, BF),
-        ("iota3", C, F32), ("xio", C, F32), ("IOTA", 400, F32), ("iotaj", 400, F32), ("mt16", 16, F32), ("D2", CS, BF), ("own", 16, BF),
+        ("iota4", C, F32), ("xio", C, F32), ("IOTA", 400, F32), ("iotaj", 400, F32), ("mt16", 16, F32), ("D2", CS, BF), ("own", 16, BF),
         ("hlf", 16, BF), ("pw", 16, F32), ("nr24", 576, BF), ("nr16", 32, F32), ("ones32", 32, F32), ("lu", 8, U16), ("ll", 8, U16),
-        ("nT", 24, F32), ("posl", 24, U16), ("posm", 24, U16), ("el4", 40, U16), ("zr", 400, BF), ("kb", 10, F32), ("ce", 10, F32),
+        ("nT", 24, F32), ("posl", 24, U16), ("posm", 24, U16), ("zr", 416, BF), ("ngc", 400, BF),
         ("cT", 24, F32), ("OH", 576, BF), ("C1", 576, BF), ("Hh", 32, F32), ("HT1", 32, F32), ("PI", 32, F32), ("G1", 64, F32),
-        ("GT", 64, F32), ("BI", 33, F32), ("G2", 24, F32), ("DD", 576, F32), ("C2", 576, F32), ("C2m", 576, F32), ("NOm", 576, BF),
-        ("SEL", 576, F32), ("rk", 24, U16), ("pir", CS, F32), ("pis", CS, F32), ("pi3", 26, U16), ("bx", 32, F32), ("be", 32, F32),
-        ("endl", 2, U16), ("tgx", 400, F32), ("LM3", 1200, BF), ("LMS", CS, BF), ("NS", CS, BF),
-        ("P0", 1200, BF), ("P1", 1200, BF), ("Z", 1200, BF), ("VV", 400, BF), ("RQ", 400, BF), ("PS", 400, F32), ("acc", 10, F32),
-        ("ac1", 1, F32), ("al", 1, U16), ("TA", 16, F32), ("FF", 17, F32), ("FD", 16, F32), ("eh", 10, F32), ("el", 10, U16),
-        ("ZS", CS, BF), ("SD1", CS, BF), ("SD2", CS, BF), ("LAST", C, F32), ("junkS", 10 * C, BF), ("junk1", 400, BF),
-        ("TT", K, F32), ("TS", K, F32), ("FZ", C, F32), ("FX", C, F32), ("FS", C, F32), ("fl24", 24, F32), ("fvV", 24, F32),
+        ("GT", 64, F32), ("BI", 33, F32), ("G2", 24, F32), ("C2", 576, BF), ("C2m", 576, BF), ("NOm", 576, BF),
+        ("SEL", 576, BF), ("rk", 24, U16), ("pir", CS, F32), ("pis", CS, F32), ("pi4", 26, U16), ("bx", 32, F32), ("be", 32, F32),
+        ("endl", 2, U16), ("tgx", 400, F32), ("LMr", C, BF), ("NS", CS, BF), ("ZS0", CS, BF),
+        ("P0", 1600, BF), ("P1", 1600, BF), ("Z", 1600, BF), ("RQ", 400, BF), ("PS", 400, F32),
+        ("ac1", 1, F32), ("al", 1, U16), ("TA", 16, F32), ("FF", 17, F32), ("FD", 16, F32), ("el", 10, U16),
+        ("ZS", CS, BF), ("SD1", CS + 1, BF), ("SD2", CS + 1, BF), ("LAST", C, F32), ("junk1", 400, BF),
+        ("TT", K, F32), ("TS", K, F32), ("FX", C, F32), ("FS", C, F32), ("fl24", 24, F32), ("fvV", 24, F32),
         ("RR", 24, F32), ("h1", 24, F32), ("d1", 24, F32), ("p1", 24, F32), ("h2", 24, F32), ("e0", 24, F32),
-        ("e1", 24, F32), ("p2", 24, F32), ("qf", 24, F32), ("fin", 24, U16)]:
+        ("e1", 24, F32), ("p2", 24, F32), ("h3", 24, F32), ("qf", 24, F32), ("fin", 24, U16)]:
     PLACE[_n] = ("pack_" + _d, _end.get(_d, 0), _w)
     _end[_d] = _end.get(_d, 0) + (_w + 31) // 32 * 32
 SCRATCH["tg2"] = ("dram", [128, 48], BF)
 for _d in _end:
     _b("pack_" + _d, _end[_d], _d)
-PSUM = ["pw0", "pw1", "pw2", "pw3", "psr", "psl", "py"]
+PSUM = ["pw0", "pw1", "pw2", "pw3", "psr", "psl", "py", "py2"]
 for _n in PSUM:
     _b(_n, 512, F32, "psum")
 
-SEMAPHORES = (["cv", "cs", "ct", "cg", "dx", "du", "dtg", "dtr", "drw", "dwc", "dws", "dv", "dol", "doc", "dos", "dy0", "dy1", "ls", "ro"]
-              + ["%s%d" % (_s, _t) for _s in ("la", "lb", "ha", "rl", "rb", "rh") for _t in range(3)])
+SEMAPHORES = (["cv", "cs", "ct", "cg", "dx", "du", "dtg", "dtr", "drw", "dwc", "dws", "dv", "dol", "doc0", "doc1", "dos", "dy0", "dy1", "ls", "ro"]
+              + ["%s%d" % (_s, _t) for _s in ("la", "lb", "lm", "ha", "rl", "rb", "rm", "rh") for _t in range(3)])
 
 
 def _bits(es):
@@ -94,9 +95,9 @@ def _relay_program(g, core, role, src, dst, T, topo):
         if role == 3:
             g.wait_ge(T.sem["rb%d" % t], n_all)
             fwd(T["lt%d" % t][:, 0:LT], T["rt%d" % t][:, 0:LT], "lb%d" % t)
-            w = 64 if t < 2 else 32
-            g.wait_ge(T.sem["rl%d" % t], n_all)
-            fwd(T["lw%d" % t][:, 0:w], T["rw%d" % t][:, 0:w], "la%d" % t)
+            for at, a, b in ((0, "rl", "la"), (32, "rm", "lm"))[:2 if t < 2 else 1]:
+                g.wait_ge(T.sem["%s%d" % (a, t)], n_all)
+                fwd(T["lw%d" % t][:, at:at + 32], T["rw%d" % t][:, at:at + 32], "%s%d" % (b, t))
         elif role == 2:
             g.wait_ge(T.sem["rh%d" % t], n_all)
             fwd(T["hls%d" % t][:, 0:K], T["rs%d" % t][:, 0:K], "ha%d" % t)
@@ -219,8 +220,8 @@ def rank_program(g, core, T, topo):
     def XT(t, b=None):
         return p("XT%d" % t, 0, 4 * C, 1, ["XT%d_%d" % (t, i) for i in range(4)]) if b is None else p("XT%d" % t, b, 4 * C, 4, "XT%d_%d" % (t, b))
 
-    def WB(n, b, a, e, parts):
-        return p("WB%d_%d" % (n, b), a, e, 1, ["W%s%d_%d" % (k, n, b) for k in parts])
+    def WB(b, a, e, parts):
+        return p("WB%d" % b, a, e, 1, ["W%s_%d" % (k, b) for k in parts])
 
     dma("s", [(T.XT0[:, 0:4 * C], T.x[:, :])], "dx", [], XT(0)[1])
     dma("y", [(T.tgT[:, :], T.tg[:, :])], "dtg", [], ["tgT"])
@@ -234,105 +235,82 @@ def rank_program(g, core, T, topo):
     iota(p("x36"), [[16, 36]])
     iota(p("m16"), [[16, 24]])
     iota(p("KC"), [[1, 24], [0, 24]])
-    iota(p("i16"), [[0, 26], [1, 16]])
     iota(p("m24"), [[1, 24]])
-    iota(p("iota3"), [[3, C]], 2)
-    iota(p("LM3"), [[0, 1200]])
-    iota(p("IOTA"), [[1, 400]])
+    iota(p("i16"), [[0, 26], [1, 16]])
     iota(p("mt16"), [[16, 16]], -64)
+    iota(p("IOTA"), [[1, 400]])
+    for b in range(4):
+        iota(WB(b, C, M1, "0"), [[0, 16]])
     op("g", lambda: g.affine_select(T.EBW[:, :], T.half[:, :], [[1, 516]], A.is_equal, 0.0, -3, -4), [p("EBW")], [p("half")])
+    iota(p("NS"), [[0, CS]], 1)
+    iota(p("ZS0"), [[0, CS]])
+    iota(p("iota4"), [[4, C]], 3)
+    iota(p("iotaj", 0, C), [[1, C]])
+    iota(p("iotaj", C, 400, 1, "iotajp"), [[0, 16]], -1)
 
     ts(p("lanei"), p("lanep"), 15, A.bitwise_and)
     fill(p("Hh"), 0.0)
     cp(p("lane"), p("lanei"))
     fill(p("ones32"), 1.0)
     ts(p("xf"), p("x36"), p("lane"), A.add)
+    fill(p("hlf"), 0.5)
     fill(p("nr24"), 1.0)
+    fill(p("BI", 0, 1, 1, "BI0"), -1.0 - MID)
+    fill(p("P0", 4 * C + 2, 4 * C + 4, 1, "P0z"), 0.0)
+    ts(p("P0", 4 * C + 1, 4 * CV, 4, "P0v"), p("hlf", 0, 15), 2.0, A.mult)
     ts(p("q1"), p("xf"), 1.0 / 24, A.mult, -11.5 / 24, A.add)
     ts(p("q3"), p("xf"), -24.0, A.mult, 552.0, A.add)
     ts(p("fl"), p("q1"), R1, A.add, R1, A.subtract)
-    fill(p("hlf"), 0.5)
     ts(p("q2"), p("fl"), -24.0, A.mult)
     ts(p("q4"), p("fl"), 577.0, A.mult)
     tt(p("q5"), p("q2"), p("xf"), A.add)
     tt(p("q6"), p("q4"), p("q3"), A.add)
     cp(p("RL"), p("q5"))
     cp(p("PL"), p("q6"))
-    ts(p("nr24", 0, 576, 24), p("nr24", 0, 576, 24), 0.0, A.mult)
-    cp(p("lu"), p("m16", 0, 8))
-    ts(p("ll"), p("m16", 0, 8), 1.0, A.add)
-    fill(p("BI", 0, 1, 1, "BI0"), 0.0)
-    fill(p("zr"), 0.0)
-    ts(p("nr16"), p("i16", 0, 32), 0.0, A.is_gt)
-    ts(p("kb"), p("m16", 0, 10), p("lane"), A.add, -160.5, A.add)
-    for i in range(3):
-        for o in ("P0", "P1"):
-            act(p(o, 400 * i, 400 * i + 400, 1, o), p("half", 0, 400), scale=0.0)
-    act(p("pir"), p("half", 0, CS), F.Identity, scale=0.0, bias=1.0 + (3 * C + 2) * STEP)
-
     ts(p("tl"), p("tgT"), 15, A.bitwise_and)
     ts(p("tg2s", 0, 24, 1, "tg2a"), p("tgT"), -192.0, A.add)
     cp(p("tg2s", 24, 48, 1, "tg2b"), p("tl"))
     dma("y", [(T.tg2[:, :], T.tg2s[:, :])], "dtr", ["tg2a", "tg2b"], ["tg2"])
     dma("y", [(T.RW[i:128:16, :], T.tg2[:, :]) for i in range(16)], "drw", ["tg2"], ["RW"])
-
     ts(p("vi"), p("tgT"), 4, A.arith_shift_right)
     tt(p("OH"), ix(p("vi"), p("RL")), p("KC"), A.is_equal)
-    quant(p("uq"), p("us"), p("UT"))
-    act(p("urs"), ix(p("us"), p("lu")))
-    cp(cast(p("ur"), dt.uint32), ix(cast(p("uq"), dt.uint32), p("lu")))
-    quant(p("xq0"), p("xs0"), XT(0))
-    mm(p("psr", 0, C), p("ur"), p("urs"), p("xq0"), p("xs0"))
-    act(p("DD"), p("OH"))
-    act(p("NOm"), ix(p("OH"), p("PL")), F.Identity, scale=-1.0, bias=1.0)
+    ts(p("nr24", 0, 576, 24), p("nr24", 0, 576, 24), 0.0, A.mult)
     scan(p("C1"), p("nr24"), p("OH"), 0.0, A.mult, A.add)
     cp(p("Hh", 0, 24), p("C1", 23, 576, 24))
     turn(p("HT1"), p("Hh"))
-    ts(p("P0", 1, 3 * C, 3, "P0r"), (p("psr", 0, C)[0], ["psr", "P0"]), 0.0, A.is_gt)
-    scan(p("P1", 0, 3 * C, 3, "P1y"), (p("P0", 1, 3 * C, 3)[0], ["P0r", "P1"]), p("zr", 0, C), -161.0, A.add, A.min)
-    act(p("uls"), ix(p("us"), p("ll")))
-    scan(p("PI"), p("nr16"), p("HT1"), 0.0, A.mult, A.add)
-    tt(p("G1", 0, 32), p("PI"), p("HT1"), A.subtract)
-    cp(cast(p("ul"), dt.uint32), ix(cast(p("uq"), dt.uint32), p("ll")))
-    mm(p("psl", 0, C), p("ul"), p("uls"), p("xq0"), p("xs0"))
-    for a in range(2):
-        ts(p("G1", 32 + 16 * a, 48 + 16 * a, 1, "G1%d" % a), p("ones32", 0, 16), p("PI", 16 * a + 15, 16 * a + 16), A.mult, 1.0, A.add)
-    turn(p("GT"), p("G1", key=["G1", "G10", "G11"]))
-    scan(p("BI", 1, 33), p("ones32"), p("GT", 32, 64), 0.0, A.mult, A.add)
-    tt(p("G2"), p("GT", 0, 24), p("BI", 0, 24, 1, ["BI", "BI0"]), A.add)
-    tt(p("DD", 0, 576, 24), p("DD", 0, 576, 24), p("G2"), A.add)
+    cp(p("lu"), p("m16", 0, 8))
+    quant(p("uq"), p("us"), p("UT"))
+    cp(cast(p("ur"), dt.uint32), ix(cast(p("uq"), dt.uint32), p("lu")))
+    for i in range(3):
+        act(p("P1", 516 * i, min(516 * i + 516, NZ), 1, "P1"), p("half", 0, min(516, NZ - 516 * i)), scale=0.0)
+    act(p("P0", 0, NZ, 4, "P0"), p("half", 0, C + 1), scale=0.0)
+    act(p("ngc"), p("half", 0, 400), F.Identity, scale=0.0, bias=-2064.0 - 80.0)
+    act(p("zr"), p("half", 0, 416), scale=0.0)
+    act(p("NOm"), ix(p("OH"), p("PL")), scale=-1000.0)
+    act(p("urs"), ix(p("us"), p("lu")))
 
     def quant_x(t):
         quant(p("xq%d" % t), p("xs%d" % t), XT(t))
 
     def planes(t, q, bs):
         for b in bs:
-            copy(q, WB(t + 1, b, 0, C, "X"), XT(t, b))
+            copy(q, WB(b, 0, C, "X"), XT(t, b))
 
     def scores(t):
         mm(p("psr", 0, C), p("ur"), p("urs"), p("xq%d" % t), p("xs%d" % t))
+
+    def scores_late(t):
         mm(p("psl", 0, C), p("ul"), p("uls"), p("xq%d" % t), p("xs%d" % t))
 
     def rise(t):
-        tt(p("P0", 1, 3 * C, 3, "P0r"), p("psr", 0, C), p("LAST"), A.is_gt)
+        tt(p("P0", 1, 4 * C, 4, "P0r"), p("psr", 0, C), p("LAST"), A.is_gt)
 
-    def count():
-        scan(p("P1", 0, 3 * C, 3, "P1y"), p("P0", 1, 3 * C, 3, "P0r"), p("zr", 0, C), -161.0, A.add, A.min)
-
-    def entries_by_counts(lo, hi):
-        for m in range(lo, hi):
-            n = C - 16 * m
-            signs(p("junkS", C * m, C * m + n, 1, "junkS%d" % m), p("P1", 48 * m, 3 * C, 3, "P1y"), p("kb", m, m + 1), p("acc", m, m + 1, 1, "acc%d" % m))
-
-    def counts_end():
-        tt(p("eh"), p("acc", 0, 10, 1, ["acc%d" % m for m in range(10)]), p("ce"), A.add)
-        ts(p("el"), p("eh"), 0.5, A.mult)
-
-    def entries_by_runs():
-        scan(p("VV", 0, CV), p("P0", 1, 3 * CV, 3, ["P0", "P0r", "P0v"]), p("zr", 0, CV), p("vini"), A.add, A.add)
-        signs(p("junk1", 0, CV), p("VV", 0, CV), p("thr"), p("ac1"))
-        ts(p("RQ", 0, CV), p("VV", 0, CV), R16, A.add, R16, A.subtract)
-        scan(p("PS", 1, 1 + CV), p("RQ", 0, CV), p("zr", 0, CV), 0.0, A.add, A.add)
+    def entries():
+        flags = p("P0", 1, 4 * CV, 4, ["P0", "P0r", "P0v"])
+        scan(p("P1", 0, 4 * CV, 4, "P1y"), flags, (p("zr", 0, CV)[0], ["zr", "P1"]), -161.0, A.add, A.min)
+        signs(p("junk1", 0, CV), p("P1", 0, 4 * CV, 4, "P1y"), p("thr"), p("ac1"))
+        scan(p("RQ", 0, CV), flags, p("zr", 0, CV), p("vini"), A.add, A.add)
+        scan(p("PS", 1, 1 + CV), p("RQ", 0, CV), p("ngc", 0, CV), 0.0, A.add, A.add)
 
     def runs_end():
         ts(p("al"), p("ac1"), float(CV), A.add, 0.5, A.mult)
@@ -342,26 +320,31 @@ def rank_program(g, core, T, topo):
         ts(p("el"), p("FD", 0, 10), 1.0 / 16, A.mult)
 
     def late(t):
-        o = p("P0", 2, 3 * C, 3, "P0l")
-        op("s", lambda: s.activation(o[0], p("psl", 0, C)[0], F.Sign, bias=-2.0 ** -118), [o], [p("psl"), p("P0", key="P0")])
+        o = p("P0", 2, 4 * C, 4, "P0l")
+        op("s", lambda: s.activation(o[0], p("psl", 0, C)[0], F.Sign, bias=-2.0 ** -118), [o], [p("psl")])
 
     def signed():
-        n = 3 * C + 3
-        scan(p("Z", 0, n), p("P0", 0, n, 1, ["P0", "P0r", "P0v", "P0l"]), p("P1", 0, n, 1, ["P1", "P1y"]), 0.0, A.mult, A.add)
+        scan(p("Z", 0, NZ), p("P0", 0, NZ, 1, ["P0", "P0r", "P0v", "P0l", "P0m", "P0z"]), p("P1", 0, NZ, 1, ["P1", "P1y"]), 0.0, A.mult, A.add)
 
     def resolve(t):
-        m = "wm%d" % t
-        tt(p("ZS"), ix(p("Z", 0, 3 * C + 3), p("pi3")), p("LMS"), A.mult)
-        scan(p("SD1"), p("NS"), p("ZS"), 0.0, A.mult, A.max)
+        if t == 0:
+            cp(ix(p("ZS0"), p("rk")), p("Z", 3, 4 * C, 4))
+        else:
+            cp(p("ZS"), ix(p("Z", 0, NZ), p("pi4")))
+        scan(p("SD1", 1, CS + 1), p("NS"), p("ZS" if t else "ZS0"), 0.0, A.mult, A.max)
+        act(p("wm%d" % t, 0, 32, 1, "wm%da" % t), ix(p("SD1", 0, CS, 1, ["SD1", "SD10"]), p("endl")))
+        send_winners(t, "a", 0, "rl")
+
+    def resolve_late(t):
+        act(p("FX"), p("Z", 1, 4 * C, 4), F.Identity, scale=-(2.0 ** -8), bias=1.0)
         if t < 2:
-            scan(p("SD2"), p("NS"), p("ZS"), 0.0, A.mult, A.min)
-        act(p(m, 0, 32, 1, m + "a"), ix(p("SD1"), p("endl")))
-        if t < 2:
-            act(p(m, 32, 64, 1, m + "b"), ix(p("SD2"), p("endl")), scale=-1.0)
+            scan(p("SD2", 1, CS + 1), p("NS"), p("ZS" if t else "ZS0"), 0.0, A.mult, A.min)
+            act(p("wm%d" % t, 32, 64, 1, "wm%db" % t), ix(p("SD2", 0, CS, 1, ["SD2", "SD20"]), p("endl")), scale=-1.0)
+            send_winners(t, "b", 32, "rm")
 
     def gather_e(t, pairs):
         for b, q in pairs:
-            copy(q, p("ET", b, None, 4, "ET%d" % b), ix(WB(t + 1, b, 0, M1, "X0"), p("el")))
+            copy(q, p("ET", b, None, 4, "ET%d" % b), ix(WB(b, 0, M1, "X0"), p("el")))
 
     def layer(t):
         quant(p("eq"), p("es"), p("ET", 0, None, 1, ["ET%d" % b for b in range(4)]))
@@ -375,9 +358,13 @@ def rank_program(g, core, T, topo):
         lane_scan(p("TS"), p("TT"), K)
         unlane(p("tm%d" % t), p("TS", 15, K, 16))
 
-    def relus():
-        for b in range(4):
-            act(p("HT", b, None, 4, "HT%d" % b), p("pw%d" % b, 0, K), F.Relu, scale=0.03125)
+    def relus(pairs):
+        for b, q in pairs:
+            o, i = p("HT", b, None, 4, "HT%d" % b), p("pw%d" % b, 0, K)
+            if q == "s":
+                act(o, i, F.Relu, scale=0.03125)
+            else:
+                ts(o, i, 0.0, A.max, 0.03125, A.mult)
 
     def quant_h(t):
         quant(p("hq%d" % t), p("hs%d" % t), p("HT", 0, None, 1, ["HT%d" % b for b in range(4)]))
@@ -405,43 +392,42 @@ def rank_program(g, core, T, topo):
         deps("g", ["tm%d" % t], [])
         send(3, T["rt%d" % t][:, 0:LT], T["tm%d" % t][:, 0:LT], "rb%d" % t)
 
-    def send_winners(t):
-        deps("g", ["wm%d%s" % (t, k) for k in "ab"], [])
-        w = 64 if t < 2 else 32
-        send(3, T["rw%d" % t][:, 0:w], T["wm%d" % t][:, 0:w], "rl%d" % t)
+    def send_winners(t, k, at, sem):
+        deps("g", ["wm%d%s" % (t, k)], [])
+        send(3, T["rw%d" % t][:, at:at + 32], T["wm%d" % t][:, at:at + 32], "%s%d" % (sem, t))
 
     def between(t):
         n = t + 1
-        act(p("FZ"), p("Z", 2, 3 * C, 3), F.Abs)
-        act(p("FX"), p("FZ"), F.Identity, scale=2.0 ** -8, bias=1.0)
-        if n >= 2:
-            lw = "lw%d" % (t - 1)
-            ts(p("h2"), p(lw, 32, 56), 0.0, A.is_gt)
-            ts(p("e0"), p(lw, 32, 56), -1.0, A.mult, float(V2 - V1), A.add)
-            for b in range(4):
-                tt(WB(n, b, V2, WEND, "B"), ix(WB(n, b, 0, M1, "X0"), p("lt%d" % (t - 1))), WB(n, b, M2, V2, "N"), A.add)
-            for b in range(4):
-                ts(WB(n, b, V2, WEND, "B"), WB(n, b, V2, WEND, "B"), 0.5, A.mult)
         if t < 2:
             act(p("LAST"), p("psr", 0, C))
+        if n >= 2:
+            for b in range(4):
+                tt(WB(b, V1 + 320 * (t - 1), V1 + 320 * (t - 1) + K, ["A%d" % (t - 1)]), p("pw%d" % b, 0, K), p("XD%d" % b), A.add)
         lane_scan(p("FS"), p("FX"), C)
         ts(p("fl24"), p("FS", 15, C, 16), p("sc"), A.mult, 1.0, A.is_gt)
-        ts(p("fvV"), p("fl24"), 160.0, A.mult, float(V1), A.add)
+        ts(p("fvV"), p("fl24"), 160.0, A.mult, float(V1 + 320 * t), A.add)
         if n >= 2:
+            older = p("lw%d" % (t - 1), 32, 56, 1, "lx%d" % (t - 1))
+            ts(p("h2"), older, 0.0, A.is_gt)
+            ts(p("e0"), older, -1.0, A.mult, -320.0, A.add)
             tt(p("e1"), p("e0"), p("fvV"), A.add)
             tt(p("p2"), p("e1"), p("h2"), A.mult)
             tt(p("RR"), p("p2"), p("cT"), A.max)
+            ts(p("h3"), p("h2"), -8192.0, A.mult)
+            tt(p("fvV"), p("fvV"), p("h3"), A.add)
 
-    def older(n):
+    def older_unpacked(t):
         for b in range(4):
-            act(WB(n, b, M2, V2, "N"), WB(n - 1, b, M1, V1, "M"))
+            act(p("XD%d" % b), ix(WB(b, 0, M1, ["X", "0"]), p("lt%d" % (t - 1))), scale=0.5)
+        for b in range(4):
+            mm(p("pw%d" % b, 0, K), p("ebq%d" % b), p("ebs%d" % b), p("hl%d" % (t - 1)), p("hls%d" % (t - 1)))
 
     def merge(n):
         t = n - 1
-        lw, lt = "lw%d" % t, "lt%d" % t
-        for b in (0, 2, 1, 3):
-            o, i = p("XG%d" % b), ix(WB(n, b, 0, M1, "X0"), p(lt))
-            if b < 2:
+        lw, lt, m, a = "lw%d" % t, "lt%d" % t, M1 + 320 * t, V1 + 320 * t
+        for b, q in ((0, "s"), (3, "v"), (1, "s"), (2, "s")):
+            o, i = p("XG%d" % b), ix(WB(b, 0, M1, ["X", "0"]), p(lt))
+            if q == "s":
                 act(o, i, scale=0.5)
             else:
                 ts(o, i, 0.5, A.mult)
@@ -449,129 +435,141 @@ def rank_program(g, core, T, topo):
             mm(p("pw%d" % b, 0, K), p("ebq%d" % b), p("ebs%d" % b), p("hl%d" % t), p("hls%d" % t))
 
         def mean(b):
-            tt(WB(n, b, V1, M2, "A"), p("pw%d" % b, 0, K), p("XG%d" % b), A.add)
+            tt(WB(b, a, a + K, ["A%d" % t]), p("pw%d" % b, 0, K), p("XG%d" % b), A.add)
 
         def move(b):
-            act(WB(n, b, M1, V1, "M"), p("pw%d" % b, 0, K), scale=2.0)
+            act(WB(b, m, m + K, ["M%d" % t]), p("pw%d" % b, 0, K), scale=2.0)
 
         def final():
-            act(p("h1"), p(lw, 0, 24), F.Sign)
+            ts(p("h1"), p(lw, 0, 24), 0.0, A.is_gt)
             tt(p("d1"), p("fvV"), p(lw, 0, 24), A.subtract)
             tt(p("p1"), p("d1"), p("h1"), A.mult)
             tt(p("qf"), p("p1"), p("cT" if n == 1 else "RR"), A.max)
             cp(p("fin"), p("qf"))
 
-        mean(0), move(1), mean(1), move(0)
+        mean(0), move(1), mean(2), move(3), mean(1), move(0)
         final()
-        mean(2), move(3), mean(3), move(2)
+        mean(3), move(2)
         for b, q in ((0, "v"), (1, "s"), (2, "v"), (3, "s")):
-            w = WB(n, b, 0, M2, "X0MA") if n == 1 else WB(n, b, 0, WEND, "X0MANB")
-            copy(q, XT(n, b), ix(w, p("fin")))
+            copy(q, XT(n, b), ix(WB(b, 0, a + K, ["X", "0"] + ["%s%d" % (k, i) for i in range(n) for k in "MA"]), p("fin")))
 
     for t in range(3):
-        for sem, n, keys in (("lb", 8, ["lt%d" % t]), ("la", 8, ["lw%d" % t]), ("ha", 24, ["hl%d" % t, "hls%d" % t])):
+        for sem, n, keys in (("lb", 8, ["lt%d" % t]), ("la", 8, ["lw%d" % t]), ("lm", 8, ["lx%d" % t]), ("ha", 24, ["hl%d" % t, "hls%d" % t])):
+            if sem == "lm" and t == 2:
+                continue
             total["%s%d" % (sem, t)] = n
             note("%s%d" % (sem, t), None, [], keys)
 
-    scan(p("C2"), p("nr24"), p("DD"), 0.0, A.mult, A.add)
-    act(p("xio"), p("iota3"), F.Identity, scale=STEP, bias=1.0)
-    entries_by_counts(0, 3)
+    quant_x(0)
+    scores(0)
+    ts(p("nr16"), p("i16", 0, 32), 0.0, A.is_gt)
+    scan(p("PI"), p("nr16"), p("HT1"), 0.0, A.mult, A.add)
+    tt(p("G1", 0, 32), p("PI"), p("HT1"), A.subtract)
+    for a in range(2):
+        ts(p("G1", 32 + 16 * a, 48 + 16 * a, 1, "G1%d" % a), p("ones32", 0, 16), p("PI", 16 * a + 15, 16 * a + 16), A.mult, 1.0, A.add)
+    turn(p("GT"), p("G1", key=["G1", "G10", "G11"]))
+    scan(p("BI", 1, 33), p("ones32"), p("GT", 32, 64), -1.0 - MID, A.mult, A.add)
+    tt(p("G2"), p("GT", 0, 24), p("BI", 0, 24, 1, ["BI", "BI0"]), A.add)
+    tt(p("OH", 0, 576, 24), p("OH", 0, 576, 24), p("G2"), A.add)
+    scan(p("C2"), p("nr24"), p("OH"), 0.0, A.mult, A.add)
+    planes(0, "s", (0, 1))
     act(p("C2m"), ix(p("C2"), p("PL")))
-    entries_by_counts(3, 10)
-    late(0)
-    ts(p("ce"), p("m16", 0, 10), 384.0, A.add)
+    ts(p("ll"), p("m16", 0, 8), 1.0, A.add)
+    ts(p("vini"), p("lane"), -1.0, A.mult, 2064.0 + 7.5, A.add)
+    ts(p("thr"), p("lane"), 16.0, A.mult, -145.5, A.add)
+    fill(p("PS", 0, 1, 1, "PS0"), 0.0)
+    fill(p("FF", 0, 1, 1, "FF0"), 0.0)
+    fill(p("tgx", C, 400, 1, "tgxp"), 1.0)
+    ts(p("P0", 1, 4 * C, 4, "P0r"), p("psr", 0, C), 0.0, A.is_gt)
+    entries()
+    runs_end()
+    planes(0, "s", (2, 3))
+    scan(p("SEL"), p("NOm"), p("C2m"), -2000.0, A.add, A.max)
+    cp(cast(p("ul"), dt.uint32), ix(cast(p("uq"), dt.uint32), p("ll")))
     ts(p("lane48"), p("lane"), 48.0, A.mult)
     ts(p("nT"), p("m24"), p("lane48"), A.add)
-    cp(p("posl"), p("nT"))
     ts(p("posm"), p("nT"), 24.0, A.add)
+    cp(p("posl"), p("nT"))
+    gather_e(0, ((0, "s"), (2, "v"), (1, "s"), (3, "v")))
+    layer(0)
+    act(p("uls"), ix(p("us"), p("ll")))
+    scores_late(0)
+    ts(p("rk"), p("SEL", 23, 576, 24), float(MID), A.add)
     ts(p("D2"), p("i16"), p("lane"), A.not_equal, 2.0, A.mult)
     ts(p("own"), p("i16", 0, 16), p("lane"), A.is_equal)
     scan(p("pw"), p("hlf"), p("own"), 0.0, A.mult, A.max)
     cp(p("sc"), p("pw", 15, 16))
     ts(p("scA"), p("sc"), 2048.0, A.mult)
-    fill(p("tgx", C, 400, 1, "tgxp"), 1.0)
-    fill(p("XT0", 4 * C, 4 * M1, 1, "XT0z"), 0.0)
-    ts(p("tgx", 0, C), ix(p("RW"), p("posl")), STEP, A.mult, 1.0 + 192 * STEP, A.add)
-    scan(p("SEL"), p("NOm"), p("C2m"), 0.0, A.mult, A.max)
-    cp(p("rk"), p("SEL", 23, 576, 24))
-    cp(ix(p("pir"), p("rk")), p("xio"))
-    counts_end()
-    for b, q in ((0, "s"), (2, "v"), (1, "s"), (3, "v")):
-        ts(p("el4", 10 * b, 10 * b + 10, 1, "el4%d" % b), p("eh"), 2.0, A.mult, float(b), A.add)
-        w = p("XT0", 0, 4 * M1, 1, XT(0)[1] + ["XT0z"])
-        copy(q, p("ET", b, None, 4, "ET%d" % b), ix(w, p("el4", 10 * b, 10 * b + 10, 1, "el4%d" % b)))
-    targets_row()
-    layer(0)
-    targets(0)
-    send_targets(0)
-    cp(p("LM3", 2, 3 * C, 3), ix(p("RW"), p("posm")))
-    relus()
-    op("s", lambda: s.activation(p("NS")[0], p("pir")[0], F.Sign, scale=-1.0, bias=1.0 + (3 * C + 1) * STEP), [p("NS")], [p("pir")])
-    quant_h(0)
-    send_codes(0)
-    lane_scan(p("pis"), p("pir"), CS)
-    unlane(p("pi3"), p("pis", 15, CS, 16))
-    ts(p("bx"), p("BI", 1, 33), STEP, A.mult, 1.0, A.add)
+    ts(p("bx"), p("BI", 1, 33), STEP, A.mult, 1.0 + (1 + MID) * STEP, A.add)
     lane_scan(p("be"), p("bx"), 32)
     unlane(p("endl"), p("be", 15, 32, 16), 1.0)
-    ts(p("LMS"), ix(p("LM3", 0, 3 * C + 3), p("pi3")), p("lane"), A.is_equal)
+    cp(ix(p("NS"), p("endl")), p("zr", 0, 32))
+    fill(p("SD1", 0, 1, 1, "SD10"), 0.0)
+    fill(p("SD2", 0, 1, 1, "SD20"), 0.0)
+    relus(((0, "s"), (1, "v"), (2, "s"), (3, "v")))
+    quant_h(0)
+    send_codes(0)
+    act(p("LMr"), ix(p("RW"), p("posm")))
+    late(0)
+    act(p("tgx", 0, C), ix(p("RW"), p("posl")), F.Identity, scale=STEP, bias=1.0 + 192 * STEP)
+    targets_row()
+    ts(p("P0", 3, 4 * C, 4, "P0m"), p("LMr"), p("lane"), A.is_equal)
     signed()
+    targets(0)
+    send_targets(0)
     resolve(0)
-    send_winners(0)
-    for n in range(1, 4):
-        for b in range(4):
-            fill(WB(n, b, C, M1, "0"), 0.0)
-    planes(0, "s", (0, 1))
-    planes(0, "v", (2, 3))
-    ts(p("vini"), p("lane"), -1.0, A.mult, -72.5, A.add)
-    ts(p("thr"), p("lane"), 15.0, A.mult, -57.0, A.add)
-    fill(p("PS", 0, 1, 1, "PS0"), 0.0)
-    fill(p("FF", 0, 1, 1, "FF0"), 0.0)
+    resolve_late(0)
     ts(p("cT"), p("m16"), p("lane"), A.add)
     for b in range(4):
         quant(p("ebq%d" % b), p("ebs%d" % b), p("EBW", 3 - b, 515 - b))
+    act(p("xio"), p("iota4"), F.Identity, scale=STEP, bias=1.0)
+    act(p("pir"), p("half", 0, CS), F.Identity, scale=0.0, bias=1.0 + (4 * C + 3) * STEP)
     between(0)
-    ts(p("P0", 3 * C + 1, 3 * CV, 3, "P0v"), p("m24", 0, 15), 0.0, A.mult, 1.0, A.add)
-    quant(p("vq"), p("vs"), p("VT"))
-    act(p("iotaj", 0, C), p("IOTA", 0, C))
-    fill(p("iotaj", C, 400, 1, "iotajp"), -1.0)
+    cp(ix(p("pir"), p("rk")), p("xio"))
+    lane_scan(p("pis"), p("pir"), CS)
+    unlane(p("pi4"), p("pis", 15, CS, 16))
 
     for t in (1, 2):
         merge(t)
         quant_x(t)
-        planes(t, "s", (0, 1))
+        planes(t, "s", (0, 1, 2))
         scores(t)
-        planes(t, "v", (2, 3))
+        scores_late(t)
+        planes(t, "v", (3,))
+        if t == 1:
+            quant(p("vq"), p("vs"), p("VT"))
         rise(t)
-        entries_by_runs()
+        entries()
         late(t)
         runs_end()
         gather_e(t, ((0, "s"), (2, "v"), (1, "s"), (3, "v")))
         targets_row()
         layer(t)
-        count()
-        targets(t)
-        send_targets(t)
-        relus()
-        older(t + 1)
         signed()
+        relus(((0, "s"), (1, "v"), (2, "s"), (3, "v")))
+        older_unpacked(t)
         quant_h(t)
         send_codes(t)
+        targets(t)
+        send_targets(t)
         resolve(t)
-        send_winners(t)
+        resolve_late(t)
         between(t)
     act(p("OLr"), ix(p("iotaj", 0, 400, 1, ["iotaj", "iotajp"]), p("el")))
     dma("y", [(T.ol[:, :], T.OLr[0:128:16, :])], "dol", ["OLr"], [])
 
     merge(3)
-    quant_x(3)
-    dma("y", [(T.oc[:, :], T.xq3[:, :].bitcast(dt.uint8))], "doc", ["xq3"], [])
-    mm(p("py", 0, C), p("vq"), p("vs"), p("xq3"), p("xs3"))
-    dma("y", [(T.osc[4 * k:4 * k + 4, :], T.xs3[32 * k:32 * k + 4, :]) for k in range(4)], "dos", ["xs3"], [])
-    cp(p("YT", 0, 192, 1, "YT0"), p("py", 0, 192))
-    act(p("YT", 192, C, 1, "YT1"), p("py", 192, C))
-    dma("y", [(T.y[:, 0:192], T.YT[:, 0:192])], "dy0", ["YT0"], [])
-    dma("s", [(T.y[:, 192:C], T.YT[:, 192:C])], "dy1", ["YT1"], [])
+    H = C // 2
+    for h, bank in enumerate(("py", "py2")):
+        a, e = H * h, H * h + H
+        quant(p("xq3", a, e, 1, "xq3%d" % h), p("xs3", a, e, 1, "xs3%d" % h), p("XT3", 4 * a, 4 * e, 1, XT(3)[1]))
+        mm(p(bank, 0, H), p("vq"), p("vs"), p("xq3", a, e, 1, "xq3%d" % h), p("xs3", a, e, 1, "xs3%d" % h))
+        dma("y", [(T.oc[:, 4 * a:4 * e], T.xq3[:, a:e].bitcast(dt.uint8))], "doc%d" % h, ["xq3%d" % h], [])
+    act(p("YT", 0, H, 1, "YT0"), p("py", 0, H))
+    cp(p("YT", H, C, 1, "YT1"), p("py2", 0, H))
+    dma("s", [(T.y[:, 0:H], T.YT[:, 0:H])], "dy0", ["YT0"], [])
+    dma("y", [(T.osc[4 * k:4 * k + 4, :], T.xs3[32 * k:32 * k + 4, :]) for k in range(4)], "dos", ["xs30", "xs31"], [])
+    dma("y", [(T.y[:, H:C], T.YT[:, H:C])], "dy1", ["YT1"], [])
     for sem in sorted(total):
         if waited.get(sem, 0) < total[sem]:
             g.wait_ge(T.sem[sem], total[sem])

from concourse.bass import DstId, RemoteDMATransfer
from concourse.mybir import dt, AluOpType as A, ActivationFunctionType as F

C, K, N = 384, 160, 8
HALF = K // 2
CV = C + 15
CS = C + 32
MID = 208
NZ = 4 * C + 4
M1, V1, WEND = 400, 560, 1360
LT = 10
STEP = 2.0 ** -11
R1 = 1.5 * 2.0 ** 23
F32, BF, I32, U16, COD, U8 = "float32", "bfloat16", "int32", "uint16", "float8_e4m3fn_x4", "uint8"
SCRATCH = {}


def _b(name, n, d, where="sbuf"):
    SCRATCH[name] = (where, [128, n], d)


for _t in range(4):
    _b("XT%d" % _t, 4 * C, BF)
    _b("xq%d" % _t, C, COD)
    _b("xs%d" % _t, C, U8)
    _b("ebq%d" % _t, 128, COD)
    _b("ebs%d" % _t, 128, U8)
    _b("XG%d" % _t, K, BF)
    _b("XD%d" % _t, K, BF)
    _b("WB%d" % _t, WEND, BF)
for _t in range(3):
    for _n, _w, _d in [("hq", K, COD), ("hs", K, U8), ("hl", K, COD), ("hls", K, U8), ("tm", LT, U16), ("wm", 64, BF),
                       ("lt", LT, U16), ("lw", 64, BF), ("rc", HALF, COD), ("rs", K, U8), ("rt", LT, U16), ("rw", 64, BF)]:
        _b("%s%d" % (_n, _t), _w, _d)
for _n, _w, _d in [
        ("UT", 512, BF), ("VT", 512, BF), ("uq", 128, COD), ("us", 128, U8), ("ur", 128, COD), ("urs", 128, U8),
        ("ul", 128, COD), ("uls", 128, U8), ("vq", 128, COD), ("vs", 128, U8), ("wq", 512, COD), ("wsp", 512, U8),
        ("tgT", 24, I32), ("RW", 2 * C, BF), ("tg2s", 48, BF), ("tl", 24, I32), ("lanep", 1, I32), ("lanei", 1, I32), ("half", 516, BF),
        ("EBW", 516, BF), ("vi", 24, I32), ("ET", 4 * K, BF), ("eq", K, COD), ("es", K, U8), ("HT", 4 * K, BF), ("OLr", K, F32),
        ("YT", C, F32)]:
    _b(_n, _w, _d)
PLACE, _end = {}, {}
for _n, _w, _d in [
        ("lane", 1, F32), ("lane48", 1, F32), ("vini", 1, F32), ("thr", 1, F32), ("sc", 1, F32), ("scA", 1, F32), ("m16", 24, F32),
        ("m24", 24, F32), ("x36", 36, F32), ("xf", 36, F32), ("q1", 36, F32), ("fl", 36, F32), ("q2", 36, F32), ("q3", 36, F32),
        ("q4", 36, F32), ("q5", 36, F32), ("q6", 36, F32), ("RL", 36, U16), ("PL", 36, U16), ("KC", 576, BF), ("i16", CS, BF),
        ("iota4", C, F32), ("xio", C, F32), ("IOTA", 400, F32), ("iotaj", 400, F32), ("mt16", 16, F32), ("D2", CS, BF), ("own", 16, BF),
        ("hlf", 16, BF), ("pw", 16, F32), ("nr24", 576, BF), ("nr16", 32, F32), ("ones32", 32, F32), ("lu", 8, U16), ("ll", 8, U16),
        ("nT", 24, F32), ("posl", 24, U16), ("posm", 24, U16), ("zr", 416, BF), ("ngc", 400, BF),
        ("cT", 24, F32), ("OH", 576, BF), ("C1", 576, BF), ("Hh", 32, F32), ("HT1", 32, F32), ("PI", 32, F32), ("G1", 64, F32),
        ("GT", 64, F32), ("BI", 33, F32), ("G2", 24, F32), ("C2", 576, BF), ("C2m", 576, BF), ("NOm", 576, BF),
        ("SEL", 576, BF), ("rk", 24, U16), ("pir", CS, F32), ("pis", CS, F32), ("pi4", 26, U16), ("bx", 32, F32), ("be", 32, F32),
        ("endl", 2, U16), ("tgx", 400, F32), ("LMr", C, BF), ("NS", CS, BF), ("ZS0", CS, BF),
        ("P0", 1600, BF), ("P1", 1600, BF), ("Z", 1600, BF), ("RQ", 400, BF), ("PS", 400, F32),
        ("ac1", 1, F32), ("al", 1, U16), ("TA", 16, F32), ("FF", 17, F32), ("FD", 16, F32), ("el", 10, U16),
        ("ZS", CS, BF), ("SD1", CS + 1, BF), ("SD2", CS + 1, BF), ("LAST", C, F32), ("junk1", 400, BF),
        ("TT", K, F32), ("TS", K, F32), ("FX", C, F32), ("FS", C, F32), ("fl24", 24, F32), ("fvV", 24, F32),
        ("RR", 24, F32), ("h1", 24, F32), ("d1", 24, F32), ("p1", 24, F32), ("h2", 24, F32), ("e0", 24, F32),
        ("e1", 24, F32), ("p2", 24, F32), ("h3", 24, F32), ("qf", 24, F32), ("fin", 24, U16)]:
    PLACE[_n] = ("pack_" + _d, _end.get(_d, 0), _w)
    _end[_d] = _end.get(_d, 0) + (_w + 31) // 32 * 32
SCRATCH["tg2"] = ("dram", [128, 48], BF)
for _d in _end:
    _b("pack_" + _d, _end[_d], _d)
PSUM = ["pw0", "pw1", "pw2", "pw3", "psr", "psl", "py", "py2"]
for _n in PSUM:
    _b(_n, 512, F32, "psum")

SEMAPHORES = (["cv", "cs", "ct", "cg", "dx", "du", "dtg", "dtr", "drw", "dwc", "dws", "dv", "dol", "doc0", "doc1", "dos", "dy0", "dy1", "ls", "ro"]
              + ["%s%d" % (_s, _t) for _s in ("la", "lb", "lm", "ha", "rl", "rb", "rm", "rh") for _t in range(3)])


def _bits(es):
    return sum(1 << e for e in es)


def _relays(rank, T, topo):
    me, dst = T.cores[rank], T.cores[(rank + 1) % N]
    able = [c for c in topo.cores_of(me) if c != me and topo.may_write(c, dst)]
    near = [c for c in able if topo.die(c) == topo.die(me)]
    far = [c for c in able if topo.die(c) != topo.die(me)]
    return near[0], far[0], near[1], far[1]


def _relay_program(g, core, role, src, dst, T, topo):
    rid, pid = topo.addr(dst, core)
    mask, n_out, n_all = topo.mask(core, dst), len(topo.engines(core, dst)), len(topo.engines(src, core))
    sent = [0]

    def fwd(out, in_, sem):
        g.remote_dma(out, in_, T.sem[sem], T.sem.ro, pid, rid, mask)
        sent[0] += n_out

    for t in range(3):
        if role == 3:
            g.wait_ge(T.sem["rb%d" % t], n_all)
            fwd(T["lt%d" % t][:, 0:LT], T["rt%d" % t][:, 0:LT], "lb%d" % t)
            for at, a, b in ((0, "rl", "la"), (32, "rm", "lm"))[:2 if t < 2 else 1]:
                g.wait_ge(T.sem["%s%d" % (a, t)], n_all)
                fwd(T["lw%d" % t][:, at:at + 32], T["rw%d" % t][:, at:at + 32], "%s%d" % (b, t))
        elif role == 2:
            g.wait_ge(T.sem["rh%d" % t], n_all)
            fwd(T["hls%d" % t][:, 0:K], T["rs%d" % t][:, 0:K], "ha%d" % t)
        else:
            g.wait_ge(T.sem["rh%d" % t], n_all // 2)
            fwd(T["hl%d" % t][:, HALF * role:HALF * role + HALF].bitcast(dt.uint8), T["rc%d" % t][:, 0:HALF].bitcast(dt.uint8), "ha%d" % t)
    g.wait_ge(T.sem.ro, sent[0])


def rank_program(g, core, T, topo):
    rank = T.rank_of(core)
    if rank is None:
        for r, c in enumerate(T.cores):
            if core in topo.cores_of(c):
                rel = _relays(r, T, topo)
                if core in rel:
                    _relay_program(g, core, rel.index(core), c, T.cores[(r + 1) % N], T, topo)
        return
    queue = {"v": g.vector, "s": g.scalar, "t": g.tensor, "g": g, "y": g.sync}
    own = {"v": "cv", "s": "cs", "t": "ct", "g": "cg"}
    total, waited, known = {}, {}, {q: {} for q in queue}
    writer, readers = {}, {}

    def deps(q, R, W):
        evs = [writer[k] for k in R if k in writer]
        for k in W:
            evs += readers.get(k, []) + ([writer[k]] if k in writer else [])
        for e in sorted(evs, key=lambda e: (-sum(e["clock"].values()), e["sem"])):
            if known[q].get(e["sem"], 0) < e["n"]:
                queue[q].wait_ge(T.sem[e["sem"]], e["n"])
                waited[e["sem"]] = max(waited.get(e["sem"], 0), e["n"])
                for s, n in e["clock"].items():
                    known[q][s] = max(known[q].get(s, 0), n)

    def note(sem, kq, R, W):
        clock = dict(known[kq]) if kq else {}
        clock[sem] = total[sem]
        ev = {"sem": sem, "n": total[sem], "clock": clock}
        for k in R:
            readers.setdefault(k, []).append(ev)
        for k in W:
            writer[k], readers[k] = ev, []

    def p(name, a=0, b=None, step=1, key=None):
        buf, at, w = PLACE[name] if name in PLACE else (name, 0, SCRATCH[name][1][1])
        return T[buf][:, at + a:at + (w if b is None else b):step], [name] if key is None else [key] if isinstance(key, str) else list(key)

    def ix(win, off):
        return win[0].indirect(off[0]), win[1] + off[1]

    def cast(x, d):
        return x[0].bitcast(d), x[1]

    def op(q, fn, outs, ins):
        R = sorted({k for o in ins for k in o[1]})
        W = sorted({k for o in outs for k in o[1]} | {k for k in R if k in PSUM})
        deps(q, R, W)
        total[own[q]] = total.get(own[q], 0) + 1
        fn().then_inc(T.sem[own[q]], 1)
        note(own[q], q, R, W)

    def dma(q, pairs, sem, R, W):
        deps(q, R, W)
        for o, i in pairs:
            queue[q].dma_start(o, i).then_inc(T.sem[sem], 16)
            total[sem] = total.get(sem, 0) + 16
        note(sem, q, R, W)

    v, s = g.vector, g.scalar

    def val(x):
        return x[0] if isinstance(x, tuple) else x

    def ts(out, in0, a, o0, b=None, o1=None):
        ins = [in0] + [x for x in (a, b) if isinstance(x, tuple)]
        if o1 is None:
            op("v", lambda: v.tensor_scalar(out[0], in0[0], val(a), None, o0), [out], ins)
        else:
            op("v", lambda: v.tensor_scalar(out[0], in0[0], val(a), val(b), o0, o1), [out], ins)

    def tt(out, a, b, o):
        op("v", lambda: v.tensor_tensor(out[0], a[0], b[0], o), [out], [a, b])

    def cp(out, in_):
        op("v", lambda: v.tensor_copy(out[0], in_[0]), [out], [in_])

    def fill(out, c):
        op("v", lambda: v.memset(out[0], c), [out], [])

    def scan(out, d0, d1, init, o0, o1):
        op("v", lambda: v.tensor_tensor_scan(out[0], d0[0], d1[0], val(init), o0, o1), [out], [d0, d1] + ([init] if isinstance(init, tuple) else []))

    def turn(out, in_):
        op("v", lambda: v.transpose(out[0], in_[0]), [out], [in_])

    def act(out, in_, func=F.Copy, **kw):
        op("s", lambda: s.activation(out[0], in_[0], func, **kw), [out], [in_])

    def signs(junk, in_, bias, accum):
        op("s", lambda: s.activation(junk[0], in_[0], F.Sign, bias=bias[0], accum_out=accum[0], scale=-1.0), [junk, accum], [in_, bias])

    def copy(q, out, in_):
        (cp if q == "v" else act)(out, in_)

    def quant(c, sc, in_):
        op("v", lambda: v.quantize_mx(c[0], sc[0], in_[0]), [c, sc], [in_])

    def mm(out, l, ls, r, rs):
        op("t", lambda: g.tensor.matmul_mx(out[0], l[0], ls[0], r[0], rs[0], True, True), [out], [l, ls, r, rs])

    def iota(out, pattern, base=0, ch=0):
        op("g", lambda: g.iota(out[0], pattern, base, ch, allow_small_or_imprecise_dtypes=True), [out], [])

    def lane_scan(out, row, n):
        scan(out, p("D2", 0, n), row, 0.0, A.mult, A.max)

    def unlane(out, rows, off=0.0):
        ts(out, rows, p("scA"), A.mult, -2048.0 - off, A.add)

    def XT(t, b=None):
        return p("XT%d" % t, 0, 4 * C, 1, ["XT%d_%d" % (t, i) for i in range(4)]) if b is None else p("XT%d" % t, b, 4 * C, 4, "XT%d_%d" % (t, b))

    def WB(b, a, e, parts):
        return p("WB%d" % b, a, e, 1, ["W%s_%d" % (k, b) for k in parts])

    dma("s", [(T.XT0[:, 0:4 * C], T.x[:, :])], "dx", [], XT(0)[1])
    dma("y", [(T.tgT[:, :], T.tg[:, :])], "dtg", [], ["tgT"])
    dma("y", [(T.UT[:, :], T.u[:, :])], "du", [], ["UT"])
    dma("y", [(T.wq[:, :].bitcast(dt.uint8), T.wc[:, :])], "dwc", [], ["wq"])
    dma("y", [(T.wsp[:, :], T.ws[:, :])], "dws", [], ["wsp"])
    dma("y", [(T.VT[:, :], T.v[:, :])], "dv", [], ["VT"])

    fill(p("half"), 0.5)
    iota(p("lanep"), [[1, 1]], 0, 1)
    iota(p("x36"), [[16, 36]])
    iota(p("m16"), [[16, 24]])
    iota(p("KC"), [[1, 24], [0, 24]])
    iota(p("m24"), [[1, 24]])
    iota(p("i16"), [[0, 26], [1, 16]])
    iota(p("mt16"), [[16, 16]], -64)
    iota(p("IOTA"), [[1, 400]])
    for b in range(4):
        iota(WB(b, C, M1, "0"), [[0, 16]])
    op("g", lambda: g.affine_select(T.EBW[:, :], T.half[:, :], [[1, 516]], A.is_equal, 0.0, -3, -4), [p("EBW")], [p("half")])
    iota(p("NS"), [[0, CS]], 1)
    iota(p("ZS0"), [[0, CS]])
    iota(p("iota4"), [[4, C]], 3)
    iota(p("iotaj", 0, C), [[1, C]])
    iota(p("iotaj", C, 400, 1, "iotajp"), [[0, 16]], -1)

    ts(p("lanei"), p("lanep"), 15, A.bitwise_and)
    fill(p("Hh"), 0.0)
    cp(p("lane"), p("lanei"))
    fill(p("ones32"), 1.0)
    ts(p("xf"), p("x36"), p("lane"), A.add)
    fill(p("hlf"), 0.5)
    fill(p("nr24"), 1.0)
    fill(p("BI", 0, 1, 1, "BI0"), -1.0 - MID)
    fill(p("P0", 4 * C + 2, 4 * C + 4, 1, "P0z"), 0.0)
    ts(p("P0", 4 * C + 1, 4 * CV, 4, "P0v"), p("hlf", 0, 15), 2.0, A.mult)
    ts(p("q1"), p("xf"), 1.0 / 24, A.mult, -11.5 / 24, A.add)
    ts(p("q3"), p("xf"), -24.0, A.mult, 552.0, A.add)
    ts(p("fl"), p("q1"), R1, A.add, R1, A.subtract)
    ts(p("q2"), p("fl"), -24.0, A.mult)
    ts(p("q4"), p("fl"), 577.0, A.mult)
    tt(p("q5"), p("q2"), p("xf"), A.add)
    tt(p("q6"), p("q4"), p("q3"), A.add)
    cp(p("RL"), p("q5"))
    cp(p("PL"), p("q6"))
    ts(p("tl"), p("tgT"), 15, A.bitwise_and)
    ts(p("tg2s", 0, 24, 1, "tg2a"), p("tgT"), -192.0, A.add)
    cp(p("tg2s", 24, 48, 1, "tg2b"), p("tl"))
    dma("y", [(T.tg2[:, :], T.tg2s[:, :])], "dtr", ["tg2a", "tg2b"], ["tg2"])
    dma("y", [(T.RW[i:128:16, :], T.tg2[:, :]) for i in range(16)], "drw", ["tg2"], ["RW"])
    ts(p("vi"), p("tgT"), 4, A.arith_shift_right)
    tt(p("OH"), ix(p("vi"), p("RL")), p("KC"), A.is_equal)
    ts(p("nr24", 0, 576, 24), p("nr24", 0, 576, 24), 0.0, A.mult)
    scan(p("C1"), p("nr24"), p("OH"), 0.0, A.mult, A.add)
    cp(p("Hh", 0, 24), p("C1", 23, 576, 24))
    turn(p("HT1"), p("Hh"))
    cp(p("lu"), p("m16", 0, 8))
    quant(p("uq"), p("us"), p("UT"))
    cp(cast(p("ur"), dt.uint32), ix(cast(p("uq"), dt.uint32), p("lu")))
    for i in range(3):
        act(p("P1", 516 * i, min(516 * i + 516, NZ), 1, "P1"), p("half", 0, min(516, NZ - 516 * i)), scale=0.0)
    act(p("P0", 0, NZ, 4, "P0"), p("half", 0, C + 1), scale=0.0)
    act(p("ngc"), p("half", 0, 400), F.Identity, scale=0.0, bias=-2064.0 - 80.0)
    act(p("zr"), p("half", 0, 416), scale=0.0)
    act(p("NOm"), ix(p("OH"), p("PL")), scale=-1000.0)
    act(p("urs"), ix(p("us"), p("lu")))

    def quant_x(t):
        quant(p("xq%d" % t), p("xs%d" % t), XT(t))

    def planes(t, q, bs):
        for b in bs:
            copy(q, WB(b, 0, C, "X"), XT(t, b))

    def scores(t):
        mm(p("psr", 0, C), p("ur"), p("urs"), p("xq%d" % t), p("xs%d" % t))

    def scores_late(t):
        mm(p("psl", 0, C), p("ul"), p("uls"), p("xq%d" % t), p("xs%d" % t))

    def rise(t):
        tt(p("P0", 1, 4 * C, 4, "P0r"), p("psr", 0, C), p("LAST"), A.is_gt)

    def entries():
        flags = p("P0", 1, 4 * CV, 4, ["P0", "P0r", "P0v"])
        scan(p("P1", 0, 4 * CV, 4, "P1y"), flags, (p("zr", 0, CV)[0], ["zr", "P1"]), -161.0, A.add, A.min)
        signs(p("junk1", 0, CV), p("P1", 0, 4 * CV, 4, "P1y"), p("thr"), p("ac1"))
        scan(p("RQ", 0, CV), flags, p("zr", 0, CV), p("vini"), A.add, A.add)
        scan(p("PS", 1, 1 + CV), p("RQ", 0, CV), p("ngc", 0, CV), 0.0, A.add, A.add)

    def runs_end():
        ts(p("al"), p("ac1"), float(CV), A.add, 0.5, A.mult)
        tt(p("TA"), ix(p("IOTA"), p("al")), p("mt16"), A.mult)
        tt(p("FF", 1, 17), ix(p("PS", 0, 400, 1, ["PS", "PS0"]), p("al")), p("TA"), A.subtract)
        tt(p("FD"), p("FF", 0, 16, 1, ["FF", "FF0"]), p("FF", 1, 17), A.subtract)
        ts(p("el"), p("FD", 0, 10), 1.0 / 16, A.mult)

    def late(t):
        o = p("P0", 2, 4 * C, 4, "P0l")
        op("s", lambda: s.activation(o[0], p("psl", 0, C)[0], F.Sign, bias=-2.0 ** -118), [o], [p("psl")])

    def signed():
        scan(p("Z", 0, NZ), p("P0", 0, NZ, 1, ["P0", "P0r", "P0v", "P0l", "P0m", "P0z"]), p("P1", 0, NZ, 1, ["P1", "P1y"]), 0.0, A.mult, A.add)

    def resolve(t):
        if t == 0:
            cp(ix(p("ZS0"), p("rk")), p("Z", 3, 4 * C, 4))
        else:
            cp(p("ZS"), ix(p("Z", 0, NZ), p("pi4")))
        scan(p("SD1", 1, CS + 1), p("NS"), p("ZS" if t else "ZS0"), 0.0, A.mult, A.max)
        act(p("wm%d" % t, 0, 32, 1, "wm%da" % t), ix(p("SD1", 0, CS, 1, ["SD1", "SD10"]), p("endl")))
        send_winners(t, "a", 0, "rl")

    def resolve_late(t):
        act(p("FX"), p("Z", 1, 4 * C, 4), F.Identity, scale=-(2.0 ** -8), bias=1.0)
        if t < 2:
            scan(p("SD2", 1, CS + 1), p("NS"), p("ZS" if t else "ZS0"), 0.0, A.mult, A.min)
            act(p("wm%d" % t, 32, 64, 1, "wm%db" % t), ix(p("SD2", 0, CS, 1, ["SD2", "SD20"]), p("endl")), scale=-1.0)
            send_winners(t, "b", 32, "rm")

    def gather_e(t, pairs):
        for b, q in pairs:
            copy(q, p("ET", b, None, 4, "ET%d" % b), ix(WB(b, 0, M1, "X0"), p("el")))

    def layer(t):
        quant(p("eq"), p("es"), p("ET", 0, None, 1, ["ET%d" % b for b in range(4)]))
        for b in range(4):
            mm(p("pw%d" % b, 0, K), p("wq", 128 * b, 128 * b + 128), p("wsp", 128 * b, 128 * b + 128), p("eq"), p("es"))

    def targets_row():
        act(p("TT"), ix(p("tgx", 0, 400, 1, ["tgx", "tgxp"]), p("el")))

    def targets(t):
        lane_scan(p("TS"), p("TT"), K)
        unlane(p("tm%d" % t), p("TS", 15, K, 16))

    def relus(pairs):
        for b, q in pairs:
            o, i = p("HT", b, None, 4, "HT%d" % b), p("pw%d" % b, 0, K)
            if q == "s":
                act(o, i, F.Relu, scale=0.03125)
            else:
                ts(o, i, 0.0, A.max, 0.03125, A.mult)

    def quant_h(t):
        quant(p("hq%d" % t), p("hs%d" % t), p("HT", 0, None, 1, ["HT%d" % b for b in range(4)]))

    rel = _relays(rank, T, topo)

    def send(i, out, in_, sem):
        rid, pid = topo.addr(rel[i], core)
        g.remote_dma(out, in_, T.sem[sem], T.sem.ls, pid, rid, topo.mask(core, rel[i]))
        total["ls"] = total.get("ls", 0) + len(topo.engines(core, rel[i]))

    def send_codes(t):
        deps("g", ["hq%d" % t, "hs%d" % t], [])
        es = topo.engines(core, rel[0])
        h, tr = len(es) // 2, []
        for i in range(2):
            rid, pid = topo.addr(rel[i], core)
            tr.append(RemoteDMATransfer(dst_ids=[DstId(rid=rid, pnc=pid)], dma_engine_mask=_bits(es[h * i:h * i + h]), remote_sem=T.sem["rh%d" % t],
                                        src=T["hq%d" % t][:, HALF * i:HALF * i + HALF].bitcast(dt.uint8), dst=T["rc%d" % t][:, 0:HALF].bitcast(dt.uint8)))
        g.remote_dma_fused(tr, local_sem=T.sem.ls)
        total["ls"] = total.get("ls", 0) + 2 * h
        send(2, T["rs%d" % t][:, 0:K], T["hs%d" % t][:, 0:K], "rh%d" % t)

    def send_targets(t):
        deps("g", ["tm%d" % t], [])
        send(3, T["rt%d" % t][:, 0:LT], T["tm%d" % t][:, 0:LT], "rb%d" % t)

    def send_winners(t, k, at, sem):
        deps("g", ["wm%d%s" % (t, k)], [])
        send(3, T["rw%d" % t][:, at:at + 32], T["wm%d" % t][:, at:at + 32], "%s%d" % (sem, t))

    def between(t):
        n = t + 1
        if t < 2:
            act(p("LAST"), p("psr", 0, C))
        if n >= 2:
            for b in range(4):
                tt(WB(b, V1 + 320 * (t - 1), V1 + 320 * (t - 1) + K, ["A%d" % (t - 1)]), p("pw%d" % b, 0, K), p("XD%d" % b), A.add)
        lane_scan(p("FS"), p("FX"), C)
        ts(p("fl24"), p("FS", 15, C, 16), p("sc"), A.mult, 1.0, A.is_gt)
        ts(p("fvV"), p("fl24"), 160.0, A.mult, float(V1 + 320 * t), A.add)
        if n >= 2:
            older = p("lw%d" % (t - 1), 32, 56, 1, "lx%d" % (t - 1))
            ts(p("h2"), older, 0.0, A.is_gt)
            ts(p("e0"), older, -1.0, A.mult, -320.0, A.add)
            tt(p("e1"), p("e0"), p("fvV"), A.add)
            tt(p("p2"), p("e1"), p("h2"), A.mult)
            tt(p("RR"), p("p2"), p("cT"), A.max)
            ts(p("h3"), p("h2"), -8192.0, A.mult)
            tt(p("fvV"), p("fvV"), p("h3"), A.add)

    def older_unpacked(t):
        for b in range(4):
            act(p("XD%d" % b), ix(WB(b, 0, M1, ["X", "0"]), p("lt%d" % (t - 1))), scale=0.5)
        for b in range(4):
            mm(p("pw%d" % b, 0, K), p("ebq%d" % b), p("ebs%d" % b), p("hl%d" % (t - 1)), p("hls%d" % (t - 1)))

    def merge(n):
        t = n - 1
        lw, lt, m, a = "lw%d" % t, "lt%d" % t, M1 + 320 * t, V1 + 320 * t
        for b, q in ((0, "s"), (3, "v"), (1, "s"), (2, "s")):
            o, i = p("XG%d" % b), ix(WB(b, 0, M1, ["X", "0"]), p(lt))
            if q == "s":
                act(o, i, scale=0.5)
            else:
                ts(o, i, 0.5, A.mult)
        for b in range(4):
            mm(p("pw%d" % b, 0, K), p("ebq%d" % b), p("ebs%d" % b), p("hl%d" % t), p("hls%d" % t))

        def mean(b):
            tt(WB(b, a, a + K, ["A%d" % t]), p("pw%d" % b, 0, K), p("XG%d" % b), A.add)

        def move(b):
            act(WB(b, m, m + K, ["M%d" % t]), p("pw%d" % b, 0, K), scale=2.0)

        def final():
            ts(p("h1"), p(lw, 0, 24), 0.0, A.is_gt)
            tt(p("d1"), p("fvV"), p(lw, 0, 24), A.subtract)
            tt(p("p1"), p("d1"), p("h1"), A.mult)
            tt(p("qf"), p("p1"), p("cT" if n == 1 else "RR"), A.max)
            cp(p("fin"), p("qf"))

        mean(0), move(1), mean(2), move(3), mean(1), move(0)
        final()
        mean(3), move(2)
        for b, q in ((0, "v"), (1, "s"), (2, "v"), (3, "s")):
            copy(q, XT(n, b), ix(WB(b, 0, a + K, ["X", "0"] + ["%s%d" % (k, i) for i in range(n) for k in "MA"]), p("fin")))

    for t in range(3):
        for sem, n, keys in (("lb", 8, ["lt%d" % t]), ("la", 8, ["lw%d" % t]), ("lm", 8, ["lx%d" % t]), ("ha", 24, ["hl%d" % t, "hls%d" % t])):
            if sem == "lm" and t == 2:
                continue
            total["%s%d" % (sem, t)] = n
            note("%s%d" % (sem, t), None, [], keys)

    quant_x(0)
    scores(0)
    ts(p("nr16"), p("i16", 0, 32), 0.0, A.is_gt)
    scan(p("PI"), p("nr16"), p("HT1"), 0.0, A.mult, A.add)
    tt(p("G1", 0, 32), p("PI"), p("HT1"), A.subtract)
    for a in range(2):
        ts(p("G1", 32 + 16 * a, 48 + 16 * a, 1, "G1%d" % a), p("ones32", 0, 16), p("PI", 16 * a + 15, 16 * a + 16), A.mult, 1.0, A.add)
    turn(p("GT"), p("G1", key=["G1", "G10", "G11"]))
    scan(p("BI", 1, 33), p("ones32"), p("GT", 32, 64), -1.0 - MID, A.mult, A.add)
    tt(p("G2"), p("GT", 0, 24), p("BI", 0, 24, 1, ["BI", "BI0"]), A.add)
    tt(p("OH", 0, 576, 24), p("OH", 0, 576, 24), p("G2"), A.add)
    scan(p("C2"), p("nr24"), p("OH"), 0.0, A.mult, A.add)
    planes(0, "s", (0, 1))
    act(p("C2m"), ix(p("C2"), p("PL")))
    ts(p("ll"), p("m16", 0, 8), 1.0, A.add)
    ts(p("vini"), p("lane"), -1.0, A.mult, 2064.0 + 7.5, A.add)
    ts(p("thr"), p("lane"), 16.0, A.mult, -145.5, A.add)
    fill(p("PS", 0, 1, 1, "PS0"), 0.0)
    fill(p("FF", 0, 1, 1, "FF0"), 0.0)
    fill(p("tgx", C, 400, 1, "tgxp"), 1.0)
    ts(p("P0", 1, 4 * C, 4, "P0r"), p("psr", 0, C), 0.0, A.is_gt)
    entries()
    runs_end()
    planes(0, "s", (2, 3))
    scan(p("SEL"), p("NOm"), p("C2m"), -2000.0, A.add, A.max)
    cp(cast(p("ul"), dt.uint32), ix(cast(p("uq"), dt.uint32), p("ll")))
    ts(p("lane48"), p("lane"), 48.0, A.mult)
    ts(p("nT"), p("m24"), p("lane48"), A.add)
    ts(p("posm"), p("nT"), 24.0, A.add)
    cp(p("posl"), p("nT"))
    gather_e(0, ((0, "s"), (2, "v"), (1, "s"), (3, "v")))
    layer(0)
    act(p("uls"), ix(p("us"), p("ll")))
    scores_late(0)
    ts(p("rk"), p("SEL", 23, 576, 24), float(MID), A.add)
    ts(p("D2"), p("i16"), p("lane"), A.not_equal, 2.0, A.mult)
    ts(p("own"), p("i16", 0, 16), p("lane"), A.is_equal)
    scan(p("pw"), p("hlf"), p("own"), 0.0, A.mult, A.max)
    cp(p("sc"), p("pw", 15, 16))
    ts(p("scA"), p("sc"), 2048.0, A.mult)
    ts(p("bx"), p("BI", 1, 33), STEP, A.mult, 1.0 + (1 + MID) * STEP, A.add)
    lane_scan(p("be"), p("bx"), 32)
    unlane(p("endl"), p("be", 15, 32, 16), 1.0)
    cp(ix(p("NS"), p("endl")), p("zr", 0, 32))
    fill(p("SD1", 0, 1, 1, "SD10"), 0.0)
    fill(p("SD2", 0, 1, 1, "SD20"), 0.0)
    relus(((0, "s"), (1, "v"), (2, "s"), (3, "v")))
    quant_h(0)
    send_codes(0)
    act(p("LMr"), ix(p("RW"), p("posm")))
    late(0)
    act(p("tgx", 0, C), ix(p("RW"), p("posl")), F.Identity, scale=STEP, bias=1.0 + 192 * STEP)
    targets_row()
    ts(p("P0", 3, 4 * C, 4, "P0m"), p("LMr"), p("lane"), A.is_equal)
    signed()
    targets(0)
    send_targets(0)
    resolve(0)
    resolve_late(0)
    ts(p("cT"), p("m16"), p("lane"), A.add)
    for b in range(4):
        quant(p("ebq%d" % b), p("ebs%d" % b), p("EBW", 3 - b, 515 - b))
    act(p("xio"), p("iota4"), F.Identity, scale=STEP, bias=1.0)
    act(p("pir"), p("half", 0, CS), F.Identity, scale=0.0, bias=1.0 + (4 * C + 3) * STEP)
    between(0)
    cp(ix(p("pir"), p("rk")), p("xio"))
    lane_scan(p("pis"), p("pir"), CS)
    unlane(p("pi4"), p("pis", 15, CS, 16))

    for t in (1, 2):
        merge(t)
        quant_x(t)
        planes(t, "s", (0, 1, 2))
        scores(t)
        scores_late(t)
        planes(t, "v", (3,))
        if t == 1:
            quant(p("vq"), p("vs"), p("VT"))
        rise(t)
        entries()
        late(t)
        runs_end()
        gather_e(t, ((0, "s"), (2, "v"), (1, "s"), (3, "v")))
        targets_row()
        layer(t)
        signed()
        relus(((0, "s"), (1, "v"), (2, "s"), (3, "v")))
        older_unpacked(t)
        quant_h(t)
        send_codes(t)
        targets(t)
        send_targets(t)
        resolve(t)
        resolve_late(t)
        between(t)
    act(p("OLr"), ix(p("iotaj", 0, 400, 1, ["iotaj", "iotajp"]), p("el")))
    dma("y", [(T.ol[:, :], T.OLr[0:128:16, :])], "dol", ["OLr"], [])

    merge(3)
    H = C // 2
    for h, bank in enumerate(("py", "py2")):
        a, e = H * h, H * h + H
        quant(p("xq3", a, e, 1, "xq3%d" % h), p("xs3", a, e, 1, "xs3%d" % h), p("XT3", 4 * a, 4 * e, 1, XT(3)[1]))
        mm(p(bank, 0, H), p("vq"), p("vs"), p("xq3", a, e, 1, "xq3%d" % h), p("xs3", a, e, 1, "xs3%d" % h))
        dma("y", [(T.oc[:, 4 * a:4 * e], T.xq3[:, a:e].bitcast(dt.uint8))], "doc%d" % h, ["xq3%d" % h], [])
    act(p("YT", 0, H, 1, "YT0"), p("py", 0, H))
    cp(p("YT", H, C, 1, "YT1"), p("py2", 0, H))
    dma("s", [(T.y[:, 0:H], T.YT[:, 0:H])], "dy0", ["YT0"], [])
    dma("y", [(T.osc[4 * k:4 * k + 4, :], T.xs3[32 * k:32 * k + 4, :]) for k in range(4)], "dos", ["xs30", "xs31"], [])
    dma("y", [(T.y[:, H:C], T.YT[:, H:C])], "dy1", ["YT1"], [])
    for sem in sorted(total):
        if waited.get(sem, 0) < total[sem]:
            g.wait_ge(T.sem[sem], total[sem])
